import numpy as np
import ml_dtypes


def mxq(x, axis, fmt="e4m3"):
    dtype, down = {"e4m3": (ml_dtypes.float8_e4m3fn, 7), "e5m2": (ml_dtypes.float8_e5m2, 14)}[fmt]
    v = np.moveaxis(np.asarray(x, np.float32).astype(ml_dtypes.bfloat16).astype(np.float64), axis, -1)
    blocks = v.reshape(v.shape[:-1] + (-1, 32))
    amax = np.abs(blocks).max(-1, keepdims=True)
    byte = np.maximum(np.where(amax > 0, np.frexp(amax)[1] - 1 + 127, 0) - down, 1)
    scale = np.exp2(byte - 127.0)
    codes = (blocks / scale).astype(np.float32).astype(dtype).astype(np.float64)
    return np.moveaxis((codes * scale).reshape(v.shape), -1, axis)


WIDE = False


def mx_kscale(k):
    if not WIDE:
        return np.ones(k)
    levels = np.array([10, -10, 5, -5, 0])
    if k % 512:
        return np.exp2(np.random.permutation(np.resize(levels, k // 32))).repeat(32)
    a = np.empty((k // 512, 16))
    for p in range(k // 512):
        a[p, :8] = np.random.permutation(np.resize(levels, 8))
        for g in range(8):
            far = levels[np.abs(levels - a[p, g]) >= 10]
            a[p, g + 8] = far[np.random.randint(len(far))]
    return np.exp2(a.ravel()).repeat(32)


def f64(x):
    return np.asarray(x).astype(np.float64)


def striped(idx):
    return np.tile(idx.reshape(-1, 16).T, (8, 1)).astype(np.uint16)


def unstriped(offs):
    return offs[:16].T.reshape(-1).astype(np.int64)


def pack_weight(w):
    k, n = w.shape
    w = f64(np.asarray(w, np.float32).astype(ml_dtypes.bfloat16)).reshape(k // 32, 32, n)
    amax = np.abs(w).max(1)
    byte = np.clip(np.where(amax > 0, np.frexp(amax)[1] - 1 + 127 - 7, 1), 1, 254)
    scaled = (w * np.exp2(127.0 - byte)[:, None, :]).reshape(k, n).astype(np.float32)
    words = np.ascontiguousarray(scaled.reshape(k // 512, 128, 4, n).transpose(0, 1, 3, 2)).astype(ml_dtypes.float8_e4m3fn).view(np.uint8)
    return words, np.ascontiguousarray(byte.astype(np.uint8).reshape(k // 512, 16, n))


def unpack_weight(words, scales):
    g, p, n, _ = words.shape
    vals = np.ascontiguousarray(words).view(ml_dtypes.float8_e4m3fn).astype(np.float64) * np.repeat(np.exp2(scales.astype(np.float64) - 127.0), 8, axis=1)[..., None]
    return vals.transpose(0, 1, 3, 2).reshape(g * 512, n)


def relu2(v):
    return np.maximum(v, 0.0) ** 2


K, T, E, C, N = 1536, 1024, 8, 128, 512


def by_expert(wq, xq):
    return np.concatenate([wq[e].T @ xq[:, e * C:(e + 1) * C] for e in range(E)], axis=1)


def setup_inputs():
    n = np.random.standard_normal
    s = mx_kscale(K)[:, None]
    packed = [pack_weight(m) for m in n((E, K, N)) / np.sqrt(K) / s[None]]
    return {
        "xT": (n((K, T)) * s).astype(np.float32),
        "w_words": np.stack([m[0] for m in packed]),
        "w_scales": np.stack([m[1] for m in packed]),
        "b": (0.3 * n((N, E))).astype(np.float32),
        "gate": np.tile(np.random.uniform(0.2, 1.0, E * C), (N, 1)).astype(np.float32),
        "offs": striped(np.random.permutation(T)[:E * C]),
        "dst": striped(np.random.permutation(T)[:E * C]),
    }


def reference(xT, w_words, w_scales, b, gate, offs, dst):
    idx = unstriped(offs)
    w = np.stack([unpack_weight(w_words[e], w_scales[e]) for e in range(E)])
    xq = mxq(f64(xT)[:, idx], 0, "e4m3")
    y = by_expert(w, xq)
    y = relu2(y + np.repeat(f64(b), C, axis=1))
    out = np.zeros((N, T))
    out[:, unstriped(dst)] = f64(gate) * y
    return out

@@ -1,0 +1,164 @@
+from contextlib import ExitStack
+
+import concourse.mybir as mybir
+
+K, T, E, C, N = 1536, 1024, 8, 128, 512
+FLOPS = 2 * K * E * C * N
+BYTES = 4 * K * T + E * K * N + E * (K // 32) * N + 4 * N * E + 4 * E * C + 2 * 2 * 128 * (E * C // 16) + 4 * N * T
+
+F32 = mybir.dt.float32
+BF16 = mybir.dt.bfloat16
+I32 = mybir.dt.int32
+U32 = mybir.dt.uint32
+U16 = mybir.dt.uint16
+U8 = mybir.dt.uint8
+FP8X4 = mybir.dt.float8_e4m3fn_x4
+RELU = mybir.ActivationFunctionType.Relu
+SQUARE = mybir.ActivationFunctionType.Square
+COPY = mybir.ActivationFunctionType.Copy
+MULT = mybir.AluOpType.mult
+
+P = 128
+PASSES = K // 512
+HALF = 512
+LIST_HALF = HALF // 16
+EXPERTS_PER_HALF = HALF // C
+
+LOADS = [
+    (0, 0, 256, 0),
+    (0, 256, 256, 0),
+    (0, 512, 512, 256),
+    (1, 0, 512, 512),
+    (1, 512, 512, 256),
+    (2, 0, 512, 512),
+    (2, 512, 512, 224),
+]
+
+
+def tile_moe_two_lin_relu2_kernel(tc, xT, w_words, w_scales, b, gate, offs, dst, out):
+    nc = tc.nc
+    with ExitStack() as ctx:
+        lists = ctx.enter_context(tc.tile_pool(name="lists", bufs=1))
+        keep = ctx.enter_context(tc.tile_pool(name="keep", bufs=1))
+        work = ctx.enter_context(tc.tile_pool(name="work", bufs=3))
+        psum = ctx.enter_context(tc.psum_pool(name="psum", bufs=1))
+
+        offs_t = lists.tile([P, T // 16], U16, name="offs_t")
+        dst_t = lists.tile([P, T // 16], U16, name="dst_t")
+
+        w_sc = keep.tile([P, E, N], U8, name="w_sc", align_bytes=64)
+        x_sc = keep.tile([P, T], U8, name="x_sc", align_bytes=64)
+        nc.vector.memset(w_sc[:].rearrange("p e n -> p (e n)").bitcast(I32), 0)
+        nc.vector.memset(x_sc[:].bitcast(I32), 0)
+
+        sc_view = w_scales.rearrange("e a (q i) n -> a i q e n", i=4)
+
+        def load_scales(queue, rows):
+            for row in rows:
+                queue.dma_start(out=w_sc[row : P : 32, :, :].bitcast(I32), in_=sc_view[row // 4, row % 4].bitcast(I32))
+
+        bias = keep.tile([P, N // P, E], F32, name="bias")
+        load_scales(nc.gpsimd, range(7))
+        nc.sync.dma_start(offs_t[:], offs)
+        x_view = xT.rearrange("(a p j) w -> a p j w", p=P, j=4)
+        raws = []
+        for n, (a, c0, width, split) in enumerate(LOADS):
+            raw = keep.tile([P, 4, width], F32, name="raw%d" % n)
+            nc.sync.dma_start(out=raw[:], in_=x_view[a, :, :, c0 : c0 + width])
+            raws.append(raw)
+        w_view = w_words.rearrange("e a p n r -> p (e a) (n r)")
+        w_tiles = {}
+        gate_t = keep.tile([P, T], F32, name="gate_t")
+        for q in range(2):
+            for pair in range(4):
+                wt = keep.tile([P, 6, 1024], U8, name="w%d_%d" % (q, pair), align_bytes=64)
+                nc.sync.dma_start(
+                    out=wt[:].bitcast(I32), in_=w_view[:, 6 * pair : 6 * pair + 6, 1024 * q : 1024 * q + 1024].bitcast(I32)
+                )
+                w_tiles[q, pair] = wt
+                if q == 0 and pair == 0:
+                    load_scales(nc.sync, range(7, 12))
+                    nc.sync.dma_start(out=bias[:], in_=b.rearrange("(g p) e -> p g e", p=P))
+                if q == 0 and pair == 1:
+                    nc.sync.dma_start(dst_t[:], dst)
+                    nc.sync.dma_start(out=gate_t[:], in_=gate[0:P, :])
+
+        codes = [keep.tile([P, T], U32, name="codes%d" % a, align_bytes=64) for a in range(PASSES)]
+        g_words = {}
+        g_bytes = {}
+        for h in range(2):
+            for a in range(PASSES):
+                g_words[h, a] = keep.tile([P, HALF], U32, name="gw%d_%d" % (h, a), align_bytes=64)
+            g_bytes[h] = keep.tile([P, HALF], U8, name="gb%d" % h, align_bytes=64)
+
+        def half_list(tile, h):
+            return tile[:, LIST_HALF * h : LIST_HALF * (h + 1)]
+
+        def gather_words(a, h):
+            nc.vector.tensor_copy(g_words[h, a][:], codes[a][:].indirect(half_list(offs_t, h)))
+
+        def gather_bytes(h):
+            nc.vector.tensor_copy(g_bytes[h][:], x_sc[:].indirect(half_list(offs_t, h)))
+
+        def interleave(copy, grouped, raw, lo, hi):
+            copy(
+                grouped[:, lo:hi, :].rearrange("p (c i) t -> p c t i", i=4),
+                raw[:, :, lo:hi].rearrange("p t (c i) -> p c t i", i=4),
+            )
+
+        for n, (a, c0, width, split) in enumerate(LOADS):
+            grouped = keep.tile([P, width, 4], BF16, name="grouped%d" % n, align_bytes=64)
+            if split > 0:
+                interleave(nc.scalar.copy, grouped, raws[n], 0, split)
+            if split < width:
+                interleave(nc.vector.tensor_copy, grouped, raws[n], split, width)
+            nc.vector.quantize_mx(
+                out=codes[a][:, c0 : c0 + width].bitcast(FP8X4),
+                scales=x_sc[4 * a : P, c0 : c0 + width],
+                in_=grouped[:].rearrange("p w j -> p (w j)"),
+            )
+            if c0 + width == T and a < PASSES - 1:
+                for h in range(2):
+                    gather_words(a, h)
+        for h in range(2):
+            gather_words(PASSES - 1, h)
+            gather_bytes(h)
+
+        windows = [keep.tile([P, T], F32, name="window%d" % g) for g in range(N // P)]
+
+        def block(g, e0, count):
+            width = C * count
+            first = C * e0
+            h = first // HALF
+            bank = psum.tile([P, width], F32, name="bank", bufs=8)
+            r = work.tile([P, width], F32, name="r")
+            for c in range(count):
+                e = e0 + c
+                slots = slice(C * e - HALF * h, C * (e + 1) - HALF * h)
+                wt = w_tiles[g // 2, e // 2]
+                for a in range(PASSES):
+                    nc.tensor.matmul_mx(
+                        out=bank[:, C * c : C * (c + 1)],
+                        lhsT=wt[:, 3 * (e % 2) + a, 512 * (g % 2) : 512 * (g % 2) + 512].bitcast(FP8X4),
+                        lhsT_scale=w_sc[4 * a : P, e, P * g : P * (g + 1)],
+                        rhs=g_words[h, a][:, slots].bitcast(FP8X4),
+                        rhs_scale=g_bytes[h][4 * a : P, slots],
+                        start=(a == 0),
+                        stop=(a == PASSES - 1),
+                    )
+            for c in range(count):
+                cols = slice(C * c, C * (c + 1))
+                nc.scalar.activation(r[:, cols], bank[:, cols], RELU, bias=bias[:, g, e0 + c : e0 + c + 1])
+            sq = work.tile([P, width], F32, name="sq")
+            nc.scalar.activation(sq[:], r[:], SQUARE)
+            nc.vector.tensor_tensor(
+                windows[g][:].indirect(dst_t[:, first // 16 : (first + width) // 16]),
+                sq[:],
+                gate_t[:, first : first + width],
+                MULT,
+            )
+
+        for g, e0, count in ((0, 0, 2), (1, 0, 2), (0, 2, 2), (1, 2, 2), (0, 4, 4), (1, 4, 4), (2, 0, 4), (3, 0, 4), (2, 4, 4), (3, 4, 4)):
+            block(g, e0, count)
+            if e0 + count == E:
+                nc.sync.dma_start(out=out[P * g : P * (g + 1), :], in_=windows[g][:])

@@ -15,24 +15,24 @@ U8 = mybir.dt.uint8
 FP8X4 = mybir.dt.float8_e4m3fn_x4
 RELU = mybir.ActivationFunctionType.Relu
 SQUARE = mybir.ActivationFunctionType.Square
-COPY = mybir.ActivationFunctionType.Copy
 MULT = mybir.AluOpType.mult
 
 P = 128
 PASSES = K // 512
-HALF = 512
-LIST_HALF = HALF // 16
-EXPERTS_PER_HALF = HALF // C
 
 LOADS = [
     (0, 0, 256, 0),
-    (0, 256, 256, 0),
-    (0, 512, 512, 256),
+    (0, 256, 256, 256),
+    (0, 512, 512, 192),
     (1, 0, 512, 512),
-    (1, 512, 512, 256),
+    (1, 512, 512, 192),
     (2, 0, 512, 512),
-    (2, 512, 512, 224),
+    (2, 512, 256, 128),
+    (2, 768, 256, 128),
 ]
+GATHERS = [(0, 2), (2, 6)]
+SCALE_GROUPS = [(0, 2), (2, 2), (4, 4)]
+BLOCKS = [(0, 0, 1), (1, 0, 2), (0, 1, 1), (1, 2, 2), (0, 2, 2), (2, 0, 4), (3, 0, 4), (0, 4, 4), (1, 4, 4), (2, 4, 4), (3, 4, 4)]
 
 
 def tile_moe_two_lin_relu2_kernel(tc, xT, w_words, w_scales, b, gate, offs, dst, out):
@@ -46,59 +46,76 @@ def tile_moe_two_lin_relu2_kernel(tc, xT, w_words, w_scales, b, gate, offs, dst,
         offs_t = lists.tile([P, T // 16], U16, name="offs_t")
         dst_t = lists.tile([P, T // 16], U16, name="dst_t")
 
-        w_sc = keep.tile([P, E, N], U8, name="w_sc", align_bytes=64)
+        w_sc = []
+        for n, (e0, count) in enumerate(SCALE_GROUPS):
+            plane = keep.tile([P, count * PASSES, N], U8, name="w_sc%d" % n, align_bytes=64)
+            nc.vector.memset(plane[:].rearrange("p j n -> p (j n)").bitcast(I32), 0)
+            w_sc.append(plane)
         x_sc = keep.tile([P, T], U8, name="x_sc", align_bytes=64)
-        nc.vector.memset(w_sc[:].rearrange("p e n -> p (e n)").bitcast(I32), 0)
         nc.vector.memset(x_sc[:].bitcast(I32), 0)
 
-        sc_view = w_scales.rearrange("e a (q i) n -> a i q e n", i=4)
+        sc_view = w_scales.rearrange("e a (q i) n -> i q (e a) n", i=4)
 
-        def load_scales(queue, rows):
-            for row in rows:
-                queue.dma_start(out=w_sc[row : P : 32, :, :].bitcast(I32), in_=sc_view[row // 4, row % 4].bitcast(I32))
+        def load_scales(n):
+            e0, count = SCALE_GROUPS[n]
+            for i in range(4):
+                nc.sync.dma_start(
+                    out=w_sc[n][i:P:32, :, :].bitcast(I32),
+                    in_=sc_view[i, :, PASSES * e0 : PASSES * (e0 + count), :].bitcast(I32),
+                )
 
-        bias = keep.tile([P, N // P, E], F32, name="bias")
-        load_scales(nc.gpsimd, range(7))
-        nc.sync.dma_start(offs_t[:], offs)
         x_view = xT.rearrange("(a p j) w -> a p j w", p=P, j=4)
         raws = []
         for n, (a, c0, width, split) in enumerate(LOADS):
             raw = keep.tile([P, 4, width], F32, name="raw%d" % n)
             nc.sync.dma_start(out=raw[:], in_=x_view[a, :, :, c0 : c0 + width])
             raws.append(raw)
+            if n == 2:
+                nc.sync.dma_start(offs_t[:], offs)
+
         w_view = w_words.rearrange("e a p n r -> p (e a) (n r)")
         w_tiles = {}
-        gate_t = keep.tile([P, T], F32, name="gate_t")
+
+        def load_words(q, pair):
+            wt = keep.tile([P, 6, 1024], U8, name="w%d_%d" % (q, pair), align_bytes=64)
+            nc.sync.dma_start(
+                out=wt[:].bitcast(I32), in_=w_view[:, 6 * pair : 6 * pair + 6, 1024 * q : 1024 * q + 1024].bitcast(I32)
+            )
+            w_tiles[q, pair] = wt
+
+        bias = keep.tile([P, N // P, E], F32, name="bias")
+        gate_t = [keep.tile([P, T // 2], F32, name="gate%d" % h) for h in range(2)]
+        load_words(0, 0)
+        load_scales(0)
+        nc.sync.dma_start(out=bias[:], in_=b.rearrange("(g p) e -> p g e", p=P))
+        nc.sync.dma_start(dst_t[:], dst)
+        nc.sync.dma_start(out=gate_t[0][:], in_=gate[0:P, 0 : T // 2])
+        load_words(0, 1)
+        load_scales(1)
+        load_words(1, 0)
+        load_words(1, 1)
+        load_scales(2)
+        nc.sync.dma_start(out=gate_t[1][:], in_=gate[0:P, T // 2 : T])
         for q in range(2):
-            for pair in range(4):
-                wt = keep.tile([P, 6, 1024], U8, name="w%d_%d" % (q, pair), align_bytes=64)
-                nc.sync.dma_start(
-                    out=wt[:].bitcast(I32), in_=w_view[:, 6 * pair : 6 * pair + 6, 1024 * q : 1024 * q + 1024].bitcast(I32)
-                )
-                w_tiles[q, pair] = wt
-                if q == 0 and pair == 0:
-                    load_scales(nc.sync, range(7, 12))
-                    nc.sync.dma_start(out=bias[:], in_=b.rearrange("(g p) e -> p g e", p=P))
-                if q == 0 and pair == 1:
-                    nc.sync.dma_start(dst_t[:], dst)
-                    nc.sync.dma_start(out=gate_t[:], in_=gate[0:P, :])
+            for pair in range(2, 4):
+                load_words(q, pair)
 
         codes = [keep.tile([P, T], U32, name="codes%d" % a, align_bytes=64) for a in range(PASSES)]
         g_words = {}
         g_bytes = {}
-        for h in range(2):
+        for h, (e0, count) in enumerate(GATHERS):
             for a in range(PASSES):
-                g_words[h, a] = keep.tile([P, HALF], U32, name="gw%d_%d" % (h, a), align_bytes=64)
-            g_bytes[h] = keep.tile([P, HALF], U8, name="gb%d" % h, align_bytes=64)
+                g_words[h, a] = keep.tile([P, C * count], U32, name="gw%d_%d" % (h, a), align_bytes=64)
+            g_bytes[h] = keep.tile([P, C * count], U8, name="gb%d" % h, align_bytes=64)
 
-        def half_list(tile, h):
-            return tile[:, LIST_HALF * h : LIST_HALF * (h + 1)]
+        def entries(tile, e0, count):
+            return tile[:, C * e0 // 16 : C * (e0 + count) // 16]
 
         def gather_words(a, h):
-            nc.vector.tensor_copy(g_words[h, a][:], codes[a][:].indirect(half_list(offs_t, h)))
+            nc.vector.tensor_copy(g_words[h, a][:], codes[a][:].indirect(entries(offs_t, *GATHERS[h])))
 
         def gather_bytes(h):
-            nc.vector.tensor_copy(g_bytes[h][:], x_sc[:].indirect(half_list(offs_t, h)))
+            nc.vector.tensor_copy(g_bytes[h][:], x_sc[:].indirect(entries(offs_t, *GATHERS[h])))
 
         def interleave(copy, grouped, raw, lo, hi):
             copy(
@@ -118,29 +135,33 @@ def tile_moe_two_lin_relu2_kernel(tc, xT, w_words, w_scales, b, gate, offs, dst,
                 in_=grouped[:].rearrange("p w j -> p (w j)"),
             )
             if c0 + width == T and a < PASSES - 1:
-                for h in range(2):
+                for h in range(len(GATHERS)):
                     gather_words(a, h)
-        for h in range(2):
+        for h in range(len(GATHERS)):
             gather_words(PASSES - 1, h)
             gather_bytes(h)
 
         windows = [keep.tile([P, T], F32, name="window%d" % g) for g in range(N // P)]
 
+        def group_of(groups, e):
+            return [n for n, (e0, count) in enumerate(groups) if e0 <= e < e0 + count][0]
+
         def block(g, e0, count):
             width = C * count
             first = C * e0
-            h = first // HALF
             bank = psum.tile([P, width], F32, name="bank", bufs=8)
             r = work.tile([P, width], F32, name="r")
             for c in range(count):
                 e = e0 + c
-                slots = slice(C * e - HALF * h, C * (e + 1) - HALF * h)
+                h = group_of(GATHERS, e)
+                s = group_of(SCALE_GROUPS, e)
+                slots = slice(C * (e - GATHERS[h][0]), C * (e + 1 - GATHERS[h][0]))
                 wt = w_tiles[g // 2, e // 2]
                 for a in range(PASSES):
                     nc.tensor.matmul_mx(
                         out=bank[:, C * c : C * (c + 1)],
                         lhsT=wt[:, 3 * (e % 2) + a, 512 * (g % 2) : 512 * (g % 2) + 512].bitcast(FP8X4),
-                        lhsT_scale=w_sc[4 * a : P, e, P * g : P * (g + 1)],
+                        lhsT_scale=w_sc[s][:, PASSES * (e - SCALE_GROUPS[s][0]) + a, P * g : P * (g + 1)],
                         rhs=g_words[h, a][:, slots].bitcast(FP8X4),
                         rhs_scale=g_bytes[h][4 * a : P, slots],
                         start=(a == 0),
@@ -151,14 +172,15 @@ def tile_moe_two_lin_relu2_kernel(tc, xT, w_words, w_scales, b, gate, offs, dst,
                 nc.scalar.activation(r[:, cols], bank[:, cols], RELU, bias=bias[:, g, e0 + c : e0 + c + 1])
             sq = work.tile([P, width], F32, name="sq")
             nc.scalar.activation(sq[:], r[:], SQUARE)
+            half = first // (T // 2)
             nc.vector.tensor_tensor(
-                windows[g][:].indirect(dst_t[:, first // 16 : (first + width) // 16]),
+                windows[g][:].indirect(entries(dst_t, e0, count)),
                 sq[:],
-                gate_t[:, first : first + width],
+                gate_t[half][:, first - half * (T // 2) : first - half * (T // 2) + width],
                 MULT,
             )
 
-        for g, e0, count in ((0, 0, 2), (1, 0, 2), (0, 2, 2), (1, 2, 2), (0, 4, 4), (1, 4, 4), (2, 0, 4), (3, 0, 4), (2, 4, 4), (3, 4, 4)):
+        for g, e0, count in BLOCKS:
             block(g, e0, count)
             if e0 + count == E:
                 nc.sync.dma_start(out=out[P * g : P * (g + 1), :], in_=windows[g][:])

@@ -20,19 +20,17 @@ MULT = mybir.AluOpType.mult
 P = 128
 PASSES = K // 512
 
-LOADS = [
-    (0, 0, 256, 0),
-    (0, 256, 256, 256),
-    (0, 512, 512, 192),
-    (1, 0, 512, 512),
-    (1, 512, 512, 192),
-    (2, 0, 512, 512),
-    (2, 512, 256, 128),
-    (2, 768, 256, 128),
-]
+CHUNK = 256
+CHUNKS = T // CHUNK
+VECTOR_SHARE = ((256, 0, 256, 160), (0, 0, 0, 192), (0, 0, 0, 160))
+QUANTS = ((2, 1, 1), (2, 2), (2, 1, 1))
 GATHERS = [(0, 2), (2, 6)]
 SCALE_GROUPS = [(0, 2), (2, 2), (4, 4)]
-BLOCKS = [(0, 0, 1), (1, 0, 2), (0, 1, 1), (1, 2, 2), (0, 2, 2), (2, 0, 4), (3, 0, 4), (0, 4, 4), (1, 4, 4), (2, 4, 4), (3, 4, 4)]
+BLOCKS = (
+    [(0, 0, 1), (1, 0, 2), (0, 1, 1), (2, 0, 2), (3, 0, 2)]
+    + [(g, 2, 2) for g in range(4)]
+    + [(0, 4, 2), (1, 4, 2), (0, 6, 2), (1, 6, 2), (2, 4, 4), (3, 4, 4)]
+)
 
 
 def tile_moe_two_lin_relu2_kernel(tc, xT, w_words, w_scales, b, gate, offs, dst, out):
@@ -40,7 +38,7 @@ def tile_moe_two_lin_relu2_kernel(tc, xT, w_words, w_scales, b, gate, offs, dst,
     with ExitStack() as ctx:
         lists = ctx.enter_context(tc.tile_pool(name="lists", bufs=1))
         keep = ctx.enter_context(tc.tile_pool(name="keep", bufs=1))
-        work = ctx.enter_context(tc.tile_pool(name="work", bufs=3))
+        work = ctx.enter_context(tc.tile_pool(name="work", bufs=4))
         psum = ctx.enter_context(tc.psum_pool(name="psum", bufs=1))
 
         offs_t = lists.tile([P, T // 16], U16, name="offs_t")
@@ -65,12 +63,13 @@ def tile_moe_two_lin_relu2_kernel(tc, xT, w_words, w_scales, b, gate, offs, dst,
                 )
 
         x_view = xT.rearrange("(a p j) w -> a p j w", p=P, j=4)
-        raws = []
-        for n, (a, c0, width, split) in enumerate(LOADS):
-            raw = keep.tile([P, 4, width], F32, name="raw%d" % n)
-            nc.sync.dma_start(out=raw[:], in_=x_view[a, :, :, c0 : c0 + width])
-            raws.append(raw)
-            if n == 2:
+        raws = {}
+        for a in range(PASSES):
+            for c in range(CHUNKS):
+                raw = keep.tile([P, 4, CHUNK], F32, name="raw%d_%d" % (a, c))
+                nc.sync.dma_start(out=raw[:], in_=x_view[a, :, :, CHUNK * c : CHUNK * (c + 1)])
+                raws[a, c] = raw
+            if a == 0:
                 nc.sync.dma_start(offs_t[:], offs)
 
         w_view = w_words.rearrange("e a p n r -> p (e a) (n r)")
@@ -84,21 +83,26 @@ def tile_moe_two_lin_relu2_kernel(tc, xT, w_words, w_scales, b, gate, offs, dst,
             w_tiles[q, pair] = wt
 
         bias = keep.tile([P, N // P, E], F32, name="bias")
-        gate_t = [keep.tile([P, T // 2], F32, name="gate%d" % h) for h in range(2)]
-        load_words(0, 0)
-        load_scales(0)
-        nc.sync.dma_start(out=bias[:], in_=b.rearrange("(g p) e -> p g e", p=P))
-        nc.sync.dma_start(dst_t[:], dst)
-        nc.sync.dma_start(out=gate_t[0][:], in_=gate[0:P, 0 : T // 2])
-        load_words(0, 1)
-        load_scales(1)
-        load_words(1, 0)
-        load_words(1, 1)
-        load_scales(2)
-        nc.sync.dma_start(out=gate_t[1][:], in_=gate[0:P, T // 2 : T])
-        for q in range(2):
-            for pair in range(2, 4):
-                load_words(q, pair)
+        gate_t = []
+
+        def load_gate(n):
+            e0, count = SCALE_GROUPS[n]
+            part = keep.tile([P, C * count], F32, name="gate%d" % n)
+            nc.sync.dma_start(out=part[:], in_=gate[0:P, C * e0 : C * (e0 + count)])
+            gate_t.append(part)
+
+        for n, (e0, count) in enumerate(SCALE_GROUPS):
+            pairs = range(e0 // 2, (e0 + count) // 2)
+            load_words(0, pairs[0])
+            load_scales(n)
+            if n == 0:
+                nc.sync.dma_start(out=bias[:], in_=b.rearrange("(g p) e -> p g e", p=P))
+                nc.sync.dma_start(dst_t[:], dst)
+            load_gate(n)
+            for q in range(2):
+                for pair in pairs:
+                    if (q, pair) not in w_tiles:
+                        load_words(q, pair)
 
         codes = [keep.tile([P, T], U32, name="codes%d" % a, align_bytes=64) for a in range(PASSES)]
         g_words = {}
@@ -117,24 +121,26 @@ def tile_moe_two_lin_relu2_kernel(tc, xT, w_words, w_scales, b, gate, offs, dst,
         def gather_bytes(h):
             nc.vector.tensor_copy(g_bytes[h][:], x_sc[:].indirect(entries(offs_t, *GATHERS[h])))
 
-        def interleave(copy, grouped, raw, lo, hi):
-            copy(
-                grouped[:, lo:hi, :].rearrange("p (c i) t -> p c t i", i=4),
-                raw[:, :, lo:hi].rearrange("p t (c i) -> p c t i", i=4),
-            )
-
-        for n, (a, c0, width, split) in enumerate(LOADS):
-            grouped = keep.tile([P, width, 4], BF16, name="grouped%d" % n, align_bytes=64)
-            if split > 0:
-                interleave(nc.scalar.copy, grouped, raws[n], 0, split)
-            if split < width:
-                interleave(nc.vector.tensor_copy, grouped, raws[n], split, width)
-            nc.vector.quantize_mx(
-                out=codes[a][:, c0 : c0 + width].bitcast(FP8X4),
-                scales=x_sc[4 * a : P, c0 : c0 + width],
-                in_=grouped[:].rearrange("p w j -> p (w j)"),
-            )
-            if c0 + width == T and a < PASSES - 1:
+        for a in range(PASSES):
+            c = 0
+            for loads in QUANTS[a]:
+                c0, width = CHUNK * c, CHUNK * loads
+                grouped = keep.tile([P, width, 4], BF16, name="grouped%d_%d" % (a, c), align_bytes=64)
+                for lo in range(0, width, CHUNK):
+                    split = CHUNK - VECTOR_SHARE[a][c]
+                    for copy, x0, x1 in ((nc.scalar.copy, 0, split), (nc.vector.tensor_copy, split, CHUNK)):
+                        if x1 > x0:
+                            copy(
+                                grouped[:, lo + x0 : lo + x1, :].rearrange("p (c i) t -> p c t i", i=4),
+                                raws[a, c][:, :, x0:x1].rearrange("p t (c i) -> p c t i", i=4),
+                            )
+                    c = c + 1
+                nc.vector.quantize_mx(
+                    out=codes[a][:, c0 : c0 + width].bitcast(FP8X4),
+                    scales=x_sc[4 * a : P, c0 : c0 + width],
+                    in_=grouped[:].rearrange("p w j -> p (w j)"),
+                )
+            if a < PASSES - 1:
                 for h in range(len(GATHERS)):
                     gather_words(a, h)
         for h in range(len(GATHERS)):
@@ -148,7 +154,6 @@ def tile_moe_two_lin_relu2_kernel(tc, xT, w_words, w_scales, b, gate, offs, dst,
 
         def block(g, e0, count):
             width = C * count
-            first = C * e0
             bank = psum.tile([P, width], F32, name="bank", bufs=8)
             r = work.tile([P, width], F32, name="r")
             for c in range(count):
@@ -172,11 +177,12 @@ def tile_moe_two_lin_relu2_kernel(tc, xT, w_words, w_scales, b, gate, offs, dst,
                 nc.scalar.activation(r[:, cols], bank[:, cols], RELU, bias=bias[:, g, e0 + c : e0 + c + 1])
             sq = work.tile([P, width], F32, name="sq")
             nc.scalar.activation(sq[:], r[:], SQUARE)
-            half = first // (T // 2)
+            s = group_of(SCALE_GROUPS, e0)
+            first = C * (e0 - SCALE_GROUPS[s][0])
             nc.vector.tensor_tensor(
                 windows[g][:].indirect(entries(dst_t, e0, count)),
                 sq[:],
-                gate_t[half][:, first - half * (T // 2) : first - half * (T // 2) + width],
+                gate_t[s][:, first : first + width],
                 MULT,
             )
 

@@ -20,10 +20,9 @@ MULT = mybir.AluOpType.mult
 P = 128
 PASSES = K // 512
 
-CHUNK = 256
-CHUNKS = T // CHUNK
-VECTOR_SHARE = ((256, 0, 256, 160), (0, 0, 0, 192), (0, 0, 0, 160))
-QUANTS = ((2, 1, 1), (2, 2), (2, 1, 1))
+LOADS = ((512, 256, 256), (320, 384, 320), (384, 384, 256))
+QUANTS = ((256, 256, 256, 256), (512, 512), (512, 256, 256))
+VECTOR_COLUMNS = (((0, 256), (512, 640), (896, 1024)), ((832, 1024),), ((704, 768), (864, 1024)))
 GATHERS = [(0, 2), (2, 6)]
 SCALE_GROUPS = [(0, 2), (2, 2), (4, 4)]
 BLOCKS = (
@@ -31,6 +30,11 @@ BLOCKS = (
     + [(g, 2, 2) for g in range(4)]
     + [(0, 4, 2), (1, 4, 2), (0, 6, 2), (1, 6, 2), (2, 4, 4), (3, 4, 4)]
 )
+
+
+def spans(widths):
+    ends = [sum(widths[: n + 1]) for n in range(len(widths))]
+    return list(zip([0] + ends[:-1], ends))
 
 
 def tile_moe_two_lin_relu2_kernel(tc, xT, w_words, w_scales, b, gate, offs, dst, out):
@@ -65,10 +69,10 @@ def tile_moe_two_lin_relu2_kernel(tc, xT, w_words, w_scales, b, gate, offs, dst,
         x_view = xT.rearrange("(a p j) w -> a p j w", p=P, j=4)
         raws = {}
         for a in range(PASSES):
-            for c in range(CHUNKS):
-                raw = keep.tile([P, 4, CHUNK], F32, name="raw%d_%d" % (a, c))
-                nc.sync.dma_start(out=raw[:], in_=x_view[a, :, :, CHUNK * c : CHUNK * (c + 1)])
-                raws[a, c] = raw
+            for lo, hi in spans(LOADS[a]):
+                raw = keep.tile([P, 4, hi - lo], F32, name="raw%d_%d" % (a, lo))
+                nc.sync.dma_start(out=raw[:], in_=x_view[a, :, :, lo:hi])
+                raws[a, lo] = raw
             if a == 0:
                 nc.sync.dma_start(offs_t[:], offs)
 
@@ -122,19 +126,22 @@ def tile_moe_two_lin_relu2_kernel(tc, xT, w_words, w_scales, b, gate, offs, dst,
             nc.vector.tensor_copy(g_bytes[h][:], x_sc[:].indirect(entries(offs_t, *GATHERS[h])))
 
         for a in range(PASSES):
-            c = 0
-            for loads in QUANTS[a]:
-                c0, width = CHUNK * c, CHUNK * loads
-                grouped = keep.tile([P, width, 4], BF16, name="grouped%d_%d" % (a, c), align_bytes=64)
-                for lo in range(0, width, CHUNK):
-                    split = CHUNK - VECTOR_SHARE[a][c]
-                    for copy, x0, x1 in ((nc.scalar.copy, 0, split), (nc.vector.tensor_copy, split, CHUNK)):
-                        if x1 > x0:
-                            copy(
-                                grouped[:, lo + x0 : lo + x1, :].rearrange("p (c i) t -> p c t i", i=4),
-                                raws[a, c][:, :, x0:x1].rearrange("p t (c i) -> p c t i", i=4),
-                            )
-                    c = c + 1
+            starts = [lo for lo, hi in spans(LOADS[a])]
+            cuts = sorted(
+                set(starts + [T] + [lo for lo, hi in spans(QUANTS[a])] + [x for span in VECTOR_COLUMNS[a] for x in span])
+            )
+            for c0, c1 in spans(QUANTS[a]):
+                width = c1 - c0
+                grouped = keep.tile([P, width, 4], BF16, name="grouped%d_%d" % (a, c0), align_bytes=64)
+                for x0, x1 in zip(cuts, cuts[1:]):
+                    if c0 <= x0 < c1:
+                        on_vector = any(lo <= x0 < hi for lo, hi in VECTOR_COLUMNS[a])
+                        copy = nc.vector.tensor_copy if on_vector else nc.scalar.copy
+                        first = max(lo for lo in starts if lo <= x0)
+                        copy(
+                            grouped[:, x0 - c0 : x1 - c0, :].rearrange("p (c i) t -> p c t i", i=4),
+                            raws[a, first][:, :, x0 - first : x1 - first].rearrange("p t (c i) -> p c t i", i=4),
+                        )
                 nc.vector.quantize_mx(
                     out=codes[a][:, c0 : c0 + width].bitcast(FP8X4),
                     scales=x_sc[4 * a : P, c0 : c0 + width],

@@ -15,7 +15,10 @@ U8 = mybir.dt.uint8
 FP8X4 = mybir.dt.float8_e4m3fn_x4
 RELU = mybir.ActivationFunctionType.Relu
 SQUARE = mybir.ActivationFunctionType.Square
+COPY = mybir.ActivationFunctionType.Copy
 MULT = mybir.AluOpType.mult
+ADD = mybir.AluOpType.add
+MAX = mybir.AluOpType.max
 
 P = 128
 PASSES = K // 512
@@ -25,11 +28,9 @@ QUANTS = ((256, 256, 256, 256), (512, 512), (512, 256, 256))
 VECTOR_COLUMNS = (((0, 256), (512, 640), (896, 1024)), ((832, 1024),), ((704, 768), (864, 1024)))
 GATHERS = [(0, 2), (2, 6)]
 SCALE_GROUPS = [(0, 2), (2, 2), (4, 4)]
-BLOCKS = (
-    [(0, 0, 1), (1, 0, 2), (0, 1, 1), (2, 0, 2), (3, 0, 2)]
-    + [(g, 2, 2) for g in range(4)]
-    + [(0, 4, 2), (1, 4, 2), (0, 6, 2), (1, 6, 2), (2, 4, 4), (3, 4, 4)]
-)
+STEPS = [((0, e), (1, e)) for e in range(E - 2)] + [((q, E - 2), (q, E - 1)) for q in range(2)]
+SCALAR_STEPS = 2
+HELD_UNTIL = 7
 
 
 def spans(widths):
@@ -77,14 +78,14 @@ def tile_moe_two_lin_relu2_kernel(tc, xT, w_words, w_scales, b, gate, offs, dst,
                 nc.sync.dma_start(offs_t[:], offs)
 
         w_view = w_words.rearrange("e a p n r -> p (e a) (n r)")
-        w_tiles = {}
+        w_tiles = []
 
-        def load_words(q, pair):
-            wt = keep.tile([P, 6, 1024], U8, name="w%d_%d" % (q, pair), align_bytes=64)
-            nc.sync.dma_start(
-                out=wt[:].bitcast(I32), in_=w_view[:, 6 * pair : 6 * pair + 6, 1024 * q : 1024 * q + 1024].bitcast(I32)
-            )
-            w_tiles[q, pair] = wt
+        def load_words(n):
+            (q0, e0), (q1, e1) = STEPS[n]
+            source = w_view[:, PASSES * e0 : PASSES * (e1 + 1), 1024 * q0 : 1024 * (q1 + 1)]
+            wt = keep.tile(list(source.shape), U8, name="w%d" % n, tag="w%d" % n, align_bytes=64)
+            nc.sync.dma_start(out=wt[:].bitcast(I32), in_=source.bitcast(I32))
+            w_tiles.append(wt)
 
         bias = keep.tile([P, N // P, E], F32, name="bias")
         gate_t = []
@@ -96,17 +97,14 @@ def tile_moe_two_lin_relu2_kernel(tc, xT, w_words, w_scales, b, gate, offs, dst,
             gate_t.append(part)
 
         for n, (e0, count) in enumerate(SCALE_GROUPS):
-            pairs = range(e0 // 2, (e0 + count) // 2)
-            load_words(0, pairs[0])
+            load_words(e0)
             load_scales(n)
             if n == 0:
                 nc.sync.dma_start(out=bias[:], in_=b.rearrange("(g p) e -> p g e", p=P))
                 nc.sync.dma_start(dst_t[:], dst)
             load_gate(n)
-            for q in range(2):
-                for pair in pairs:
-                    if (q, pair) not in w_tiles:
-                        load_words(q, pair)
+            for m in range(e0 + 1, e0 + count):
+                load_words(m)
 
         codes = [keep.tile([P, T], U32, name="codes%d" % a, align_bytes=64) for a in range(PASSES)]
         g_words = {}
@@ -159,41 +157,89 @@ def tile_moe_two_lin_relu2_kernel(tc, xT, w_words, w_scales, b, gate, offs, dst,
         def group_of(groups, e):
             return [n for n, (e0, count) in enumerate(groups) if e0 <= e < e0 + count][0]
 
-        def block(g, e0, count):
-            width = C * count
-            bank = psum.tile([P, width], F32, name="bank", bufs=8)
-            r = work.tile([P, width], F32, name="r")
-            for c in range(count):
-                e = e0 + c
+        def products(n, second):
+            bank = psum.tile([P, 2, C], F32, name="bank", bufs=8)
+            (q0, e0), (q1, e1) = STEPS[n]
+            for u, (q, e) in enumerate(STEPS[n]):
+                g = 2 * q + second
                 h = group_of(GATHERS, e)
                 s = group_of(SCALE_GROUPS, e)
                 slots = slice(C * (e - GATHERS[h][0]), C * (e + 1 - GATHERS[h][0]))
-                wt = w_tiles[g // 2, e // 2]
+                first = 512 * (g - 2 * q0)
                 for a in range(PASSES):
                     nc.tensor.matmul_mx(
-                        out=bank[:, C * c : C * (c + 1)],
-                        lhsT=wt[:, 3 * (e % 2) + a, 512 * (g % 2) : 512 * (g % 2) + 512].bitcast(FP8X4),
+                        out=bank[:, u, :],
+                        lhsT=w_tiles[n][:, PASSES * (e - e0) + a, first : first + 512].bitcast(FP8X4),
                         lhsT_scale=w_sc[s][:, PASSES * (e - SCALE_GROUPS[s][0]) + a, P * g : P * (g + 1)],
                         rhs=g_words[h, a][:, slots].bitcast(FP8X4),
                         rhs_scale=g_bytes[h][4 * a : P, slots],
                         start=(a == 0),
                         stop=(a == PASSES - 1),
                     )
-            for c in range(count):
-                cols = slice(C * c, C * (c + 1))
-                nc.scalar.activation(r[:, cols], bank[:, cols], RELU, bias=bias[:, g, e0 + c : e0 + c + 1])
-            sq = work.tile([P, width], F32, name="sq")
-            nc.scalar.activation(sq[:], r[:], SQUARE)
+            return bank
+
+        def gate_of(e0, count):
             s = group_of(SCALE_GROUPS, e0)
             first = C * (e0 - SCALE_GROUPS[s][0])
-            nc.vector.tensor_tensor(
-                windows[g][:].indirect(entries(dst_t, e0, count)),
-                sq[:],
-                gate_t[s][:, first : first + width],
-                MULT,
-            )
+            return gate_t[s][:, first : first + C * count]
 
-        for g, e0, count in BLOCKS:
-            block(g, e0, count)
-            if e0 + count == E:
-                nc.sync.dma_start(out=out[P * g : P * (g + 1), :], in_=windows[g][:])
+        def step_gate(n):
+            (q0, e0), (q1, e1) = STEPS[n]
+            if e0 == e1:
+                return gate_of(e0, 1).unsqueeze(1).to_broadcast([P, 2, C])
+            return gate_of(e0, 2).rearrange("p (u c) -> p u c", c=C)
+
+        def step_bias(n, second):
+            (q0, e0), (q1, e1) = STEPS[n]
+            if e0 == e1:
+                return bias[:, second::2, e0]
+            return bias[:, 2 * q0 + second, e0 : e0 + 2]
+
+        def relu_on_scalar(r, n, second):
+            bank = products(n, second)
+            for u in range(2):
+                nc.scalar.activation(r[:, u, :], bank[:, u, :], RELU, bias=step_bias(n, second)[:, u : u + 1])
+
+        def begin(n):
+            if n < SCALAR_STEPS:
+                r = work.tile([P, 2, 2, C], F32, name="r_all")
+                for second in (1, 0):
+                    relu_on_scalar(r[:, second], n, second)
+                return r, None, None
+            bank = products(n, 1)
+            pre = work.tile([P, 2, C], F32, name="pre")
+            nc.vector.tensor_tensor(pre[:], bank[:], step_bias(n, 1).unsqueeze(2).to_broadcast([P, 2, C]), ADD)
+            clipped = work.tile([P, 2, C], F32, name="clipped")
+            nc.vector.scalar_tensor_tensor(clipped[:], pre[:], 0.0, step_gate(n), MAX, MULT)
+            r = work.tile([P, 2, C], F32, name="r")
+            relu_on_scalar(r, n, 0)
+            return r, pre, clipped
+
+        def finish(n, r, pre, clipped):
+            tag = "w%d" % (n + 1) if n < HELD_UNTIL else "ready%d" % n
+            ready = keep.tile([P, 3, 2, C], F32, name="ready%d" % n, tag=tag, align_bytes=64)
+            sq, gated = ready[:, 0], ready[:, 2]
+            if n < SCALAR_STEPS:
+                nc.scalar.activation(ready[:, 0:2], r[:], SQUARE)
+                nc.vector.tensor_tensor(gated, ready[:, 1], step_gate(n), MULT)
+            else:
+                nc.scalar.activation(sq, r[:], SQUARE)
+                nc.vector.tensor_tensor(gated, clipped[:], pre[:], MULT)
+            (q0, e0), (q1, e1) = STEPS[n]
+            if e0 == e1:
+                parts = [(q, e0, 1, sq[:, q, :], gated[:, q, :]) for q in range(2)]
+            else:
+                parts = [(q0, e0, 2, sq.rearrange("p u c -> p (u c)"), gated.rearrange("p u c -> p (u c)"))]
+            for q, e, count, left, right in parts:
+                places = entries(dst_t, e, count)
+                nc.vector.tensor_tensor(windows[2 * q][:].indirect(places), left, gate_of(e, count), MULT)
+                nc.scalar.activation(windows[2 * q + 1][:].indirect(places), right, COPY)
+                if e + count == E:
+                    for g in (2 * q, 2 * q + 1):
+                        nc.sync.dma_start(out=out[P * g : P * (g + 1), :], in_=windows[g][:])
+
+        begun = begin(0)
+        for n in range(len(STEPS)):
+            following = begin(n + 1) if n + 1 < len(STEPS) else None
+            finish(n, *begun)
+            begun = following

@@ -27,10 +27,11 @@ LOADS = ((512, 256, 256), (320, 384, 320), (384, 384, 256))
 QUANTS = ((256, 256, 256, 256), (512, 512), (512, 256, 256))
 VECTOR_COLUMNS = (((0, 256), (512, 640), (896, 1024)), ((832, 1024),), ((704, 768), (864, 1024)))
 GATHERS = [(0, 2), (2, 6)]
-SCALE_GROUPS = [(0, 2), (2, 2), (4, 4)]
+SCALE_GROUPS = [(0, 2), (2, 2), (4, 2), (6, 2)]
+GATE_GROUPS = [(0, 4), (4, 4)]
 STEPS = [((0, e), (1, e)) for e in range(E - 2)] + [((q, E - 2), (q, E - 1)) for q in range(2)]
 SCALAR_STEPS = 2
-HELD_UNTIL = 7
+HELD = range(1, 7)
 
 
 def spans(widths):
@@ -91,20 +92,24 @@ def tile_moe_two_lin_relu2_kernel(tc, xT, w_words, w_scales, b, gate, offs, dst,
         gate_t = []
 
         def load_gate(n):
-            e0, count = SCALE_GROUPS[n]
+            e0, count = GATE_GROUPS[n]
             part = keep.tile([P, C * count], F32, name="gate%d" % n)
             nc.sync.dma_start(out=part[:], in_=gate[0:P, C * e0 : C * (e0 + count)])
             gate_t.append(part)
 
-        for n, (e0, count) in enumerate(SCALE_GROUPS):
-            load_words(e0)
-            load_scales(n)
-            if n == 0:
-                nc.sync.dma_start(out=bias[:], in_=b.rearrange("(g p) e -> p g e", p=P))
-                nc.sync.dma_start(dst_t[:], dst)
-            load_gate(n)
-            for m in range(e0 + 1, e0 + count):
-                load_words(m)
+        load_words(0)
+        nc.sync.dma_start(out=bias[:], in_=b.rearrange("(g p) e -> p g e", p=P))
+        nc.sync.dma_start(dst_t[:], dst)
+        load_gate(0)
+        load_scales(0)
+        load_scales(1)
+        for n in range(1, 5):
+            load_words(n)
+        load_gate(1)
+        load_scales(2)
+        load_scales(3)
+        for n in range(5, 8):
+            load_words(n)
 
         codes = [keep.tile([P, T], U32, name="codes%d" % a, align_bytes=64) for a in range(PASSES)]
         g_words = {}
@@ -179,8 +184,8 @@ def tile_moe_two_lin_relu2_kernel(tc, xT, w_words, w_scales, b, gate, offs, dst,
             return bank
 
         def gate_of(e0, count):
-            s = group_of(SCALE_GROUPS, e0)
-            first = C * (e0 - SCALE_GROUPS[s][0])
+            s = group_of(GATE_GROUPS, e0)
+            first = C * (e0 - GATE_GROUPS[s][0])
             return gate_t[s][:, first : first + C * count]
 
         def step_gate(n):
@@ -205,18 +210,23 @@ def tile_moe_two_lin_relu2_kernel(tc, xT, w_words, w_scales, b, gate, offs, dst,
                 r = work.tile([P, 2, 2, C], F32, name="r_all")
                 for second in (1, 0):
                     relu_on_scalar(r[:, second], n, second)
-                return r, None, None
+                return r, None
+            r = work.tile([P, 2, C], F32, name="r")
+            relu_on_scalar(r, n, 0)
             bank = products(n, 1)
             pre = work.tile([P, 2, C], F32, name="pre")
             nc.vector.tensor_tensor(pre[:], bank[:], step_bias(n, 1).unsqueeze(2).to_broadcast([P, 2, C]), ADD)
+            return r, pre
+
+        def clip(n, pre):
+            if pre is None:
+                return None
             clipped = work.tile([P, 2, C], F32, name="clipped")
             nc.vector.scalar_tensor_tensor(clipped[:], pre[:], 0.0, step_gate(n), MAX, MULT)
-            r = work.tile([P, 2, C], F32, name="r")
-            relu_on_scalar(r, n, 0)
-            return r, pre, clipped
+            return clipped
 
         def finish(n, r, pre, clipped):
-            tag = "w%d" % (n + 1) if n < HELD_UNTIL else "ready%d" % n
+            tag = "w%d" % (n + 1) if n in HELD else "ready%d" % n
             ready = keep.tile([P, 3, 2, C], F32, name="ready%d" % n, tag=tag, align_bytes=64)
             sq, gated = ready[:, 0], ready[:, 2]
             if n < SCALAR_STEPS:
@@ -225,6 +235,9 @@ def tile_moe_two_lin_relu2_kernel(tc, xT, w_words, w_scales, b, gate, offs, dst,
             else:
                 nc.scalar.activation(sq, r[:], SQUARE)
                 nc.vector.tensor_tensor(gated, clipped[:], pre[:], MULT)
+            return sq, gated
+
+        def scatter(n, sq, gated):
             (q0, e0), (q1, e1) = STEPS[n]
             if e0 == e1:
                 parts = [(q, e0, 1, sq[:, q, :], gated[:, q, :]) for q in range(2)]
@@ -238,8 +251,12 @@ def tile_moe_two_lin_relu2_kernel(tc, xT, w_words, w_scales, b, gate, offs, dst,
                     for g in (2 * q, 2 * q + 1):
                         nc.sync.dma_start(out=out[P * g : P * (g + 1), :], in_=windows[g][:])
 
-        begun = begin(0)
+        r, pre = begin(0)
+        clipped = clip(0, pre)
         for n in range(len(STEPS)):
-            following = begin(n + 1) if n + 1 < len(STEPS) else None
-            finish(n, *begun)
-            begun = following
+            last = n + 1 == len(STEPS)
+            next_r, next_pre = (None, None) if last else begin(n + 1)
+            sq, gated = finish(n, r, pre, clipped)
+            clipped = clip(n + 1, next_pre)
+            scatter(n, sq, gated)
+            r, pre = next_r, next_pre

@@ -27,10 +27,11 @@ LOADS = ((512, 256, 256), (320, 384, 320), (384, 384, 256))
 QUANTS = ((256, 256, 256, 256), (512, 512), (512, 256, 256))
 VECTOR_COLUMNS = (((0, 256), (512, 640), (896, 1024)), ((832, 1024),), ((704, 768), (864, 1024)))
 GATHERS = [(0, 2), (2, 6)]
-SCALE_GROUPS = [(0, 2), (2, 2), (4, 2), (6, 2)]
-GATE_GROUPS = [(0, 4), (4, 4)]
-STEPS = [((0, e), (1, e)) for e in range(E - 2)] + [((q, E - 2), (q, E - 1)) for q in range(2)]
-SCALAR_STEPS = 2
+SCALE_GROUPS = [(0, 2), (2, 2), (4, 4)]
+STEPS = [(range(4), range(e, e + 1)) for e in range(E - 2)] + [(range(2 * q, 2 * q + 2), range(E - 2, E)) for q in range(2)]
+VECTOR_ROWS = range(0, 1)
+SCALAR_ROWS = range(1, 4)
+SCALAR_STEPS = 1
 HELD = range(1, 7)
 
 
@@ -82,8 +83,8 @@ def tile_moe_two_lin_relu2_kernel(tc, xT, w_words, w_scales, b, gate, offs, dst,
         w_tiles = []
 
         def load_words(n):
-            (q0, e0), (q1, e1) = STEPS[n]
-            source = w_view[:, PASSES * e0 : PASSES * (e1 + 1), 1024 * q0 : 1024 * (q1 + 1)]
+            rows, experts = STEPS[n]
+            source = w_view[:, PASSES * experts.start : PASSES * experts.stop, 512 * rows.start : 512 * rows.stop]
             wt = keep.tile(list(source.shape), U8, name="w%d" % n, tag="w%d" % n, align_bytes=64)
             nc.sync.dma_start(out=wt[:].bitcast(I32), in_=source.bitcast(I32))
             w_tiles.append(wt)
@@ -92,24 +93,20 @@ def tile_moe_two_lin_relu2_kernel(tc, xT, w_words, w_scales, b, gate, offs, dst,
         gate_t = []
 
         def load_gate(n):
-            e0, count = GATE_GROUPS[n]
+            e0, count = SCALE_GROUPS[n]
             part = keep.tile([P, C * count], F32, name="gate%d" % n)
             nc.sync.dma_start(out=part[:], in_=gate[0:P, C * e0 : C * (e0 + count)])
             gate_t.append(part)
 
-        load_words(0)
-        nc.sync.dma_start(out=bias[:], in_=b.rearrange("(g p) e -> p g e", p=P))
-        nc.sync.dma_start(dst_t[:], dst)
-        load_gate(0)
-        load_scales(0)
-        load_scales(1)
-        for n in range(1, 5):
-            load_words(n)
-        load_gate(1)
-        load_scales(2)
-        load_scales(3)
-        for n in range(5, 8):
-            load_words(n)
+        for n, (e0, count) in enumerate(SCALE_GROUPS):
+            load_words(e0)
+            load_scales(n)
+            if n == 0:
+                nc.sync.dma_start(out=bias[:], in_=b.rearrange("(g p) e -> p g e", p=P))
+                nc.sync.dma_start(dst_t[:], dst)
+            load_gate(n)
+            for m in range(e0 + 1, e0 + count):
+                load_words(m)
 
         codes = [keep.tile([P, T], U32, name="codes%d" % a, align_bytes=64) for a in range(PASSES)]
         g_words = {}
@@ -162,94 +159,101 @@ def tile_moe_two_lin_relu2_kernel(tc, xT, w_words, w_scales, b, gate, offs, dst,
         def group_of(groups, e):
             return [n for n, (e0, count) in enumerate(groups) if e0 <= e < e0 + count][0]
 
-        def products(n, second):
-            bank = psum.tile([P, 2, C], F32, name="bank", bufs=8)
-            (q0, e0), (q1, e1) = STEPS[n]
-            for u, (q, e) in enumerate(STEPS[n]):
-                g = 2 * q + second
-                h = group_of(GATHERS, e)
-                s = group_of(SCALE_GROUPS, e)
-                slots = slice(C * (e - GATHERS[h][0]), C * (e + 1 - GATHERS[h][0]))
-                first = 512 * (g - 2 * q0)
-                for a in range(PASSES):
-                    nc.tensor.matmul_mx(
-                        out=bank[:, u, :],
-                        lhsT=w_tiles[n][:, PASSES * (e - e0) + a, first : first + 512].bitcast(FP8X4),
-                        lhsT_scale=w_sc[s][:, PASSES * (e - SCALE_GROUPS[s][0]) + a, P * g : P * (g + 1)],
-                        rhs=g_words[h, a][:, slots].bitcast(FP8X4),
-                        rhs_scale=g_bytes[h][4 * a : P, slots],
-                        start=(a == 0),
-                        stop=(a == PASSES - 1),
-                    )
+        def shared(n, owned):
+            common = [g for g in owned if g in STEPS[n][0]]
+            return range(common[0], common[-1] + 1, owned.step) if common else range(0)
+
+        def products(n, rows):
+            experts = STEPS[n][1]
+            bank = psum.tile([P, len(rows), len(experts), C], F32, name="bank", bufs=8)
+            for u, g in enumerate(rows):
+                for v, e in enumerate(experts):
+                    h = group_of(GATHERS, e)
+                    s = group_of(SCALE_GROUPS, e)
+                    slots = slice(C * (e - GATHERS[h][0]), C * (e + 1 - GATHERS[h][0]))
+                    first = 512 * (g - STEPS[n][0].start)
+                    for a in range(PASSES):
+                        nc.tensor.matmul_mx(
+                            out=bank[:, u, v, :],
+                            lhsT=w_tiles[n][:, PASSES * v + a, first : first + 512].bitcast(FP8X4),
+                            lhsT_scale=w_sc[s][:, PASSES * (e - SCALE_GROUPS[s][0]) + a, P * g : P * (g + 1)],
+                            rhs=g_words[h, a][:, slots].bitcast(FP8X4),
+                            rhs_scale=g_bytes[h][4 * a : P, slots],
+                            start=(a == 0),
+                            stop=(a == PASSES - 1),
+                        )
             return bank
 
-        def gate_of(e0, count):
-            s = group_of(GATE_GROUPS, e0)
-            first = C * (e0 - GATE_GROUPS[s][0])
-            return gate_t[s][:, first : first + C * count]
+        def gate_of(experts):
+            s = group_of(SCALE_GROUPS, experts.start)
+            first = C * (experts.start - SCALE_GROUPS[s][0])
+            return gate_t[s][:, first : first + C * len(experts)]
 
-        def step_gate(n):
-            (q0, e0), (q1, e1) = STEPS[n]
-            if e0 == e1:
-                return gate_of(e0, 1).unsqueeze(1).to_broadcast([P, 2, C])
-            return gate_of(e0, 2).rearrange("p (u c) -> p u c", c=C)
+        def gate_over(n, rows):
+            experts = STEPS[n][1]
+            return gate_of(experts).unsqueeze(1).to_broadcast([P, len(rows), C * len(experts)])
 
-        def step_bias(n, second):
-            (q0, e0), (q1, e1) = STEPS[n]
-            if e0 == e1:
-                return bias[:, second::2, e0]
-            return bias[:, 2 * q0 + second, e0 : e0 + 2]
-
-        def relu_on_scalar(r, n, second):
-            bank = products(n, second)
-            for u in range(2):
-                nc.scalar.activation(r[:, u, :], bank[:, u, :], RELU, bias=step_bias(n, second)[:, u : u + 1])
+        def relu_on_scalar(n, rows, name):
+            experts = STEPS[n][1]
+            bank = products(n, rows)
+            r = work.tile([P, len(rows), C * len(experts)], F32, name=name)
+            for u, g in enumerate(rows):
+                for v, e in enumerate(experts):
+                    nc.scalar.activation(r[:, u, C * v : C * (v + 1)], bank[:, u, v, :], RELU, bias=bias[:, g, e : e + 1])
+            return r
 
         def begin(n):
+            experts = STEPS[n][1]
+            mine, theirs = shared(n, VECTOR_ROWS), shared(n, SCALAR_ROWS)
             if n < SCALAR_STEPS:
-                r = work.tile([P, 2, 2, C], F32, name="r_all")
-                for second in (1, 0):
-                    relu_on_scalar(r[:, second], n, second)
-                return r, None
-            r = work.tile([P, 2, C], F32, name="r")
-            relu_on_scalar(r, n, 0)
-            bank = products(n, 1)
-            pre = work.tile([P, 2, C], F32, name="pre")
-            nc.vector.tensor_tensor(pre[:], bank[:], step_bias(n, 1).unsqueeze(2).to_broadcast([P, 2, C]), ADD)
+                pre = relu_on_scalar(n, theirs, "pre")
+                return relu_on_scalar(n, mine, "r"), pre
+            r = relu_on_scalar(n, mine, "r") if mine else None
+            bank = products(n, theirs)
+            pre = work.tile([P, len(theirs), C * len(experts)], F32, name="pre")
+            nc.vector.tensor_tensor(
+                pre[:].rearrange("p u (v c) -> p u v c", c=C),
+                bank[:],
+                bias[:, theirs.start : theirs.stop : theirs.step, experts.start : experts.stop]
+                .unsqueeze(3)
+                .to_broadcast([P, len(theirs), len(experts), C]),
+                ADD,
+            )
             return r, pre
 
         def clip(n, pre):
-            if pre is None:
+            if n < SCALAR_STEPS or pre is None:
                 return None
-            clipped = work.tile([P, 2, C], F32, name="clipped")
-            nc.vector.scalar_tensor_tensor(clipped[:], pre[:], 0.0, step_gate(n), MAX, MULT)
+            clipped = work.tile(list(pre.shape), F32, name="clipped")
+            nc.vector.scalar_tensor_tensor(clipped[:], pre[:], 0.0, gate_over(n, shared(n, SCALAR_ROWS)), MAX, MULT)
             return clipped
 
         def finish(n, r, pre, clipped):
+            mine, theirs = shared(n, VECTOR_ROWS), shared(n, SCALAR_ROWS)
+            width = C * len(STEPS[n][1])
             tag = "w%d" % (n + 1) if n in HELD else "ready%d" % n
-            ready = keep.tile([P, 3, 2, C], F32, name="ready%d" % n, tag=tag, align_bytes=64)
-            sq, gated = ready[:, 0], ready[:, 2]
+            ready = keep.tile([P, len(mine) + 2 * len(theirs), width], F32, name="ready%d" % n, tag=tag, align_bytes=64)
+            sq, gated = ready[:, 0 : len(mine), :], ready[:, len(mine) : len(mine) + len(theirs), :]
             if n < SCALAR_STEPS:
-                nc.scalar.activation(ready[:, 0:2], r[:], SQUARE)
-                nc.vector.tensor_tensor(gated, ready[:, 1], step_gate(n), MULT)
+                ungated = ready[:, len(mine) + len(theirs) :, :]
+                nc.scalar.activation(ungated, pre[:], SQUARE)
+                nc.vector.tensor_tensor(gated, ungated, gate_over(n, theirs), MULT)
             else:
-                nc.scalar.activation(sq, r[:], SQUARE)
                 nc.vector.tensor_tensor(gated, clipped[:], pre[:], MULT)
+            if mine:
+                nc.scalar.activation(sq, r[:], SQUARE)
             return sq, gated
 
         def scatter(n, sq, gated):
-            (q0, e0), (q1, e1) = STEPS[n]
-            if e0 == e1:
-                parts = [(q, e0, 1, sq[:, q, :], gated[:, q, :]) for q in range(2)]
-            else:
-                parts = [(q0, e0, 2, sq.rearrange("p u c -> p (u c)"), gated.rearrange("p u c -> p (u c)"))]
-            for q, e, count, left, right in parts:
-                places = entries(dst_t, e, count)
-                nc.vector.tensor_tensor(windows[2 * q][:].indirect(places), left, gate_of(e, count), MULT)
-                nc.scalar.activation(windows[2 * q + 1][:].indirect(places), right, COPY)
-                if e + count == E:
-                    for g in (2 * q, 2 * q + 1):
-                        nc.sync.dma_start(out=out[P * g : P * (g + 1), :], in_=windows[g][:])
+            experts = STEPS[n][1]
+            places = entries(dst_t, experts.start, len(experts))
+            for u, g in enumerate(shared(n, VECTOR_ROWS)):
+                nc.vector.tensor_tensor(windows[g][:].indirect(places), sq[:, u, :], gate_of(experts), MULT)
+            for u, g in enumerate(shared(n, SCALAR_ROWS)):
+                nc.scalar.activation(windows[g][:].indirect(places), gated[:, u, :], COPY)
+            if experts.stop == E:
+                for g in STEPS[n][0]:
+                    nc.sync.dma_start(out=out[P * g : P * (g + 1), :], in_=windows[g][:])
 
         r, pre = begin(0)
         clipped = clip(0, pre)

@@ -29,9 +29,7 @@ VECTOR_COLUMNS = (((0, 256), (512, 640), (896, 1024)), ((832, 1024),), ((704, 76
 GATHERS = [(0, 2), (2, 6)]
 SCALE_GROUPS = [(0, 2), (2, 2), (4, 4)]
 STEPS = [(range(4), range(e, e + 1)) for e in range(E - 2)] + [(range(2 * q, 2 * q + 2), range(E - 2, E)) for q in range(2)]
-VECTOR_ROWS = range(0, 1)
-SCALAR_ROWS = range(1, 4)
-SCALAR_STEPS = 1
+SCALAR_STEPS = E - 2
 HELD = range(1, 7)
 
 
@@ -160,8 +158,8 @@ def tile_moe_two_lin_relu2_kernel(tc, xT, w_words, w_scales, b, gate, offs, dst,
             return [n for n, (e0, count) in enumerate(groups) if e0 <= e < e0 + count][0]
 
         def shared(n, owned):
-            common = [g for g in owned if g in STEPS[n][0]]
-            return range(common[0], common[-1] + 1, owned.step) if common else range(0)
+            rows = STEPS[n][0]
+            return rows[:-1] if owned == "vector" else rows[-1:]
 
         def products(n, rows):
             experts = STEPS[n][1]
@@ -204,7 +202,7 @@ def tile_moe_two_lin_relu2_kernel(tc, xT, w_words, w_scales, b, gate, offs, dst,
 
         def begin(n):
             experts = STEPS[n][1]
-            mine, theirs = shared(n, VECTOR_ROWS), shared(n, SCALAR_ROWS)
+            mine, theirs = shared(n, "vector"), shared(n, "scalar")
             if n < SCALAR_STEPS:
                 pre = relu_on_scalar(n, theirs, "pre")
                 return relu_on_scalar(n, mine, "r"), pre
@@ -225,11 +223,11 @@ def tile_moe_two_lin_relu2_kernel(tc, xT, w_words, w_scales, b, gate, offs, dst,
             if n < SCALAR_STEPS or pre is None:
                 return None
             clipped = work.tile(list(pre.shape), F32, name="clipped")
-            nc.vector.scalar_tensor_tensor(clipped[:], pre[:], 0.0, gate_over(n, shared(n, SCALAR_ROWS)), MAX, MULT)
+            nc.vector.scalar_tensor_tensor(clipped[:], pre[:], 0.0, gate_over(n, shared(n, "scalar")), MAX, MULT)
             return clipped
 
         def finish(n, r, pre, clipped):
-            mine, theirs = shared(n, VECTOR_ROWS), shared(n, SCALAR_ROWS)
+            mine, theirs = shared(n, "vector"), shared(n, "scalar")
             width = C * len(STEPS[n][1])
             tag = "w%d" % (n + 1) if n in HELD else "ready%d" % n
             ready = keep.tile([P, len(mine) + 2 * len(theirs), width], F32, name="ready%d" % n, tag=tag, align_bytes=64)
@@ -247,9 +245,9 @@ def tile_moe_two_lin_relu2_kernel(tc, xT, w_words, w_scales, b, gate, offs, dst,
         def scatter(n, sq, gated):
             experts = STEPS[n][1]
             places = entries(dst_t, experts.start, len(experts))
-            for u, g in enumerate(shared(n, VECTOR_ROWS)):
+            for u, g in enumerate(shared(n, "vector")):
                 nc.vector.tensor_tensor(windows[g][:].indirect(places), sq[:, u, :], gate_of(experts), MULT)
-            for u, g in enumerate(shared(n, SCALAR_ROWS)):
+            for u, g in enumerate(shared(n, "scalar")):
                 nc.scalar.activation(windows[g][:].indirect(places), gated[:, u, :], COPY)
             if experts.stop == E:
                 for g in STEPS[n][0]:

@@ -27,10 +27,10 @@ LOADS = ((512, 256, 256), (320, 384, 320), (384, 384, 256))
 QUANTS = ((256, 256, 256, 256), (512, 512), (512, 256, 256))
 VECTOR_COLUMNS = (((0, 256), (512, 640), (896, 1024)), ((832, 1024),), ((704, 768), (864, 1024)))
 GATHERS = [(0, 2), (2, 6)]
-SCALE_GROUPS = [(0, 2), (2, 2), (4, 4)]
+SCALE_GROUPS = [(0, 2), (2, 2), (4, 2), (6, 2)]
 STEPS = [(range(4), range(e, e + 1)) for e in range(E - 2)] + [(range(2 * q, 2 * q + 2), range(E - 2, E)) for q in range(2)]
-SCALAR_STEPS = E - 2
-HELD = range(1, 7)
+WHOLE_STEPS = E - 2
+SPARE = 4 * C
 
 
 def spans(widths):
@@ -152,14 +152,10 @@ def tile_moe_two_lin_relu2_kernel(tc, xT, w_words, w_scales, b, gate, offs, dst,
             gather_words(PASSES - 1, h)
             gather_bytes(h)
 
-        windows = [keep.tile([P, T], F32, name="window%d" % g) for g in range(N // P)]
+        windows = [keep.tile([P, T + SPARE * (g == 3)], F32, name="window%d" % g) for g in range(N // P)]
 
         def group_of(groups, e):
             return [n for n, (e0, count) in enumerate(groups) if e0 <= e < e0 + count][0]
-
-        def shared(n, owned):
-            rows = STEPS[n][0]
-            return rows[:-1] if owned == "vector" else rows[-1:]
 
         def products(n, rows):
             experts = STEPS[n][1]
@@ -187,78 +183,83 @@ def tile_moe_two_lin_relu2_kernel(tc, xT, w_words, w_scales, b, gate, offs, dst,
             first = C * (experts.start - SCALE_GROUPS[s][0])
             return gate_t[s][:, first : first + C * len(experts)]
 
-        def gate_over(n, rows):
-            experts = STEPS[n][1]
-            return gate_of(experts).unsqueeze(1).to_broadcast([P, len(rows), C * len(experts)])
-
-        def relu_on_scalar(n, rows, name):
-            experts = STEPS[n][1]
+        def relu_on_scalar(r, n, rows):
             bank = products(n, rows)
-            r = work.tile([P, len(rows), C * len(experts)], F32, name=name)
             for u, g in enumerate(rows):
-                for v, e in enumerate(experts):
+                for v, e in enumerate(STEPS[n][1]):
                     nc.scalar.activation(r[:, u, C * v : C * (v + 1)], bank[:, u, v, :], RELU, bias=bias[:, g, e : e + 1])
-            return r
 
-        def begin(n):
-            experts = STEPS[n][1]
-            mine, theirs = shared(n, "vector"), shared(n, "scalar")
-            if n < SCALAR_STEPS:
-                pre = relu_on_scalar(n, theirs, "pre")
-                return relu_on_scalar(n, mine, "r"), pre
-            r = relu_on_scalar(n, mine, "r") if mine else None
-            bank = products(n, theirs)
-            pre = work.tile([P, len(theirs), C * len(experts)], F32, name="pre")
-            nc.vector.tensor_tensor(
-                pre[:].rearrange("p u (v c) -> p u v c", c=C),
-                bank[:],
-                bias[:, theirs.start : theirs.stop : theirs.step, experts.start : experts.stop]
-                .unsqueeze(3)
-                .to_broadcast([P, len(theirs), len(experts), C]),
-                ADD,
-            )
-            return r, pre
-
-        def clip(n, pre):
-            if n < SCALAR_STEPS or pre is None:
-                return None
-            clipped = work.tile(list(pre.shape), F32, name="clipped")
-            nc.vector.scalar_tensor_tensor(clipped[:], pre[:], 0.0, gate_over(n, shared(n, "scalar")), MAX, MULT)
-            return clipped
-
-        def finish(n, r, pre, clipped):
-            mine, theirs = shared(n, "vector"), shared(n, "scalar")
-            width = C * len(STEPS[n][1])
-            tag = "w%d" % (n + 1) if n in HELD else "ready%d" % n
-            ready = keep.tile([P, len(mine) + 2 * len(theirs), width], F32, name="ready%d" % n, tag=tag, align_bytes=64)
-            sq, gated = ready[:, 0 : len(mine), :], ready[:, len(mine) : len(mine) + len(theirs), :]
-            if n < SCALAR_STEPS:
-                ungated = ready[:, len(mine) + len(theirs) :, :]
-                nc.scalar.activation(ungated, pre[:], SQUARE)
-                nc.vector.tensor_tensor(gated, ungated, gate_over(n, theirs), MULT)
-            else:
-                nc.vector.tensor_tensor(gated, clipped[:], pre[:], MULT)
-            if mine:
-                nc.scalar.activation(sq, r[:], SQUARE)
-            return sq, gated
-
-        def scatter(n, sq, gated):
-            experts = STEPS[n][1]
+        def scatter_on_vector(g, experts, sq):
             places = entries(dst_t, experts.start, len(experts))
-            for u, g in enumerate(shared(n, "vector")):
-                nc.vector.tensor_tensor(windows[g][:].indirect(places), sq[:, u, :], gate_of(experts), MULT)
-            for u, g in enumerate(shared(n, "scalar")):
-                nc.scalar.activation(windows[g][:].indirect(places), gated[:, u, :], COPY)
-            if experts.stop == E:
-                for g in STEPS[n][0]:
-                    nc.sync.dma_start(out=out[P * g : P * (g + 1), :], in_=windows[g][:])
+            nc.vector.tensor_tensor(windows[g][:].indirect(places), sq, gate_of(experts), MULT)
 
-        r, pre = begin(0)
-        clipped = clip(0, pre)
-        for n in range(len(STEPS)):
-            last = n + 1 == len(STEPS)
-            next_r, next_pre = (None, None) if last else begin(n + 1)
-            sq, gated = finish(n, r, pre, clipped)
-            clipped = clip(n + 1, next_pre)
-            scatter(n, sq, gated)
-            r, pre = next_r, next_pre
+        def scatter_on_scalar(g, experts, gated):
+            places = entries(dst_t, experts.start, len(experts))
+            nc.scalar.activation(windows[g][:].indirect(places), gated, COPY)
+
+        def spare(g, rows, width):
+            return windows[g][:, T : T + rows * width].rearrange("p (u c) -> p u c", c=width)
+
+        waiting = None
+        for n in range(WHOLE_STEPS):
+            rows, experts = STEPS[n]
+            second = n % 2
+            if not second:
+                sq = keep.tile([P, 4, 2 * C], F32, name="sq%d" % n)
+            if waiting:
+                r = spare(3, 4, C)
+            else:
+                r = work.tile([P, 4, C], F32, name="r")[:, :, :]
+            relu_on_scalar(r[:, 0:2], n, rows[0:2])
+            relu_on_scalar(r[:, 2:4], n, rows[2:4])
+            mine = sq[:, :, C * second : C * (second + 1)]
+            nc.scalar.activation(mine, r, SQUARE)
+            if waiting:
+                scatter_on_scalar(3, *waiting)
+                waiting = None
+            if second:
+                pair = range(n - 1, n + 1)
+                gated = keep.tile([P, 2 * C], F32, name="gated%d" % n)
+                nc.vector.tensor_tensor(gated[:], sq[:, 3, :], gate_of(pair), MULT)
+                waiting = (pair, gated[:])
+            for g in rows[:-1]:
+                scatter_on_vector(g, experts, mine[:, g, :])
+        scatter_on_scalar(3, *waiting)
+
+        def store(g):
+            nc.sync.dma_start(out=out[P * g : P * (g + 1), :], in_=windows[g][:, 0:T])
+
+        experts = STEPS[WHOLE_STEPS][1]
+        width = C * len(experts)
+        r = keep.tile([P, 2, width], F32, name="r_lower")
+        relu_on_scalar(r[:, 0:1], WHOLE_STEPS, range(0, 1))
+        relu_on_scalar(r[:, 1:2], WHOLE_STEPS, range(1, 2))
+        sq = keep.tile([P, 2, width], F32, name="sq_lower")
+        nc.scalar.activation(sq[:], r[:], SQUARE)
+        gated = keep.tile([P, width], F32, name="gated_lower")
+        nc.vector.tensor_tensor(gated[:], sq[:, 1, :], gate_of(experts), MULT)
+        scatter_on_vector(0, experts, sq[:, 0, :])
+        scatter_on_scalar(1, experts, gated[:])
+        store(0)
+        store(1)
+
+        bank = products(WHOLE_STEPS + 1, range(3, 4))
+        pre = keep.tile([P, width], F32, name="pre")
+        nc.vector.tensor_tensor(
+            pre[:].rearrange("p (v c) -> p v c", c=C),
+            bank[:, 0],
+            bias[:, 3, experts.start : experts.stop].unsqueeze(2).to_broadcast([P, len(experts), C]),
+            ADD,
+        )
+        clipped = keep.tile([P, width], F32, name="clipped")
+        nc.vector.scalar_tensor_tensor(clipped[:], pre[:], 0.0, gate_of(experts), MAX, MULT)
+        gated = keep.tile([P, width], F32, name="gated_upper")
+        nc.vector.tensor_tensor(gated[:], clipped[:], pre[:], MULT)
+        r = spare(3, 1, width)
+        relu_on_scalar(r, WHOLE_STEPS + 1, range(2, 3))
+        sq = keep.tile([P, width], F32, name="sq_upper")
+        nc.scalar.activation(sq[:], r[:, 0], SQUARE)
+        scatter_on_vector(2, experts, sq[:])
+        scatter_on_scalar(3, experts, gated[:])
+        store(2)
+        store(3)

@@ -1,6 +1,7 @@
 from contextlib import ExitStack
 
 import concourse.mybir as mybir
+from concourse.masks import make_identity
 
 K, T, E, C, N = 1536, 1024, 8, 128, 512
 FLOPS = 2 * K * E * C * N
@@ -29,8 +30,8 @@ VECTOR_COLUMNS = (((0, 256), (512, 640), (896, 1024)), ((832, 1024),), ((704, 76
 GATHERS = [(0, 2), (2, 6)]
 SCALE_GROUPS = [(0, 2), (2, 2), (4, 2), (6, 2)]
 STEPS = [(range(4), range(e, e + 1)) for e in range(E - 2)] + [(range(2 * q, 2 * q + 2), range(E - 2, E)) for q in range(2)]
-WHOLE_STEPS = E - 2
-SPARE = 4 * C
+SCALAR_STEPS = 1
+HELD = range(1, 7)
 
 
 def spans(widths):
@@ -87,22 +88,19 @@ def tile_moe_two_lin_relu2_kernel(tc, xT, w_words, w_scales, b, gate, offs, dst,
             nc.sync.dma_start(out=wt[:].bitcast(I32), in_=source.bitcast(I32))
             w_tiles.append(wt)
 
-        bias = keep.tile([P, N // P, E], F32, name="bias")
-        gate_t = []
-
-        def load_gate(n):
-            e0, count = SCALE_GROUPS[n]
-            part = keep.tile([P, C * count], F32, name="gate%d" % n)
-            nc.sync.dma_start(out=part[:], in_=gate[0:P, C * e0 : C * (e0 + count)])
-            gate_t.append(part)
+        identity = keep.tile([P, P], F32, name="identity")
+        make_identity(nc, identity[:])
+        gate_rows = keep.tile([P, E], F32, name="gate_rows")
+        nc.sync.dma_start(out=gate_rows[:], in_=gate[0, :].rearrange("(k r) -> k r", r=E))
+        bias_rows = keep.tile([P, 3 * E + P], F32, name="bias_rows")
+        nc.gpsimd.memset(bias_rows[:, 4 * E :], 0.0)
+        nc.sync.dma_start(out=bias_rows[:, 0 : 4 * E], in_=b.rearrange("(p j) e -> p (j e)", j=4))
 
         for n, (e0, count) in enumerate(SCALE_GROUPS):
             load_words(e0)
             load_scales(n)
             if n == 0:
-                nc.sync.dma_start(out=bias[:], in_=b.rearrange("(g p) e -> p g e", p=P))
                 nc.sync.dma_start(dst_t[:], dst)
-            load_gate(n)
             for m in range(e0 + 1, e0 + count):
                 load_words(m)
 
@@ -152,10 +150,36 @@ def tile_moe_two_lin_relu2_kernel(tc, xT, w_words, w_scales, b, gate, offs, dst,
             gather_words(PASSES - 1, h)
             gather_bytes(h)
 
-        windows = [keep.tile([P, T + SPARE * (g == 3)], F32, name="window%d" % g) for g in range(N // P)]
+        turned = psum.tile([P, 4, P], F32, name="bank", bufs=8)
+        for j in range(4):
+            nc.tensor.transpose(turned[:, j, :], bias_rows[:, E * j : E * j + P], identity[:])
+        by_expert = keep.tile([P, P, 4], F32, name="by_expert")
+        nc.scalar.copy(by_expert[:], turned[:].rearrange("e j p -> e p j"))
+        spread = []
+        for h in range(2):
+            half = psum.tile([P, 4, P], F32, name="bank", bufs=8)
+            for r in range(4):
+                nc.tensor.transpose(half[:, r, :], gate_rows[:, 4 * h + r : 4 * h + r + 1].to_broadcast([P, P]), identity[:])
+            spread.append(half)
+        back = psum.tile([P, N // P, P], F32, name="bank", bufs=8)
+        for g in range(N // P):
+            nc.tensor.transpose(back[:, g, :], by_expert[:].rearrange("e p j -> e (p j)")[:, P * g : P * (g + 1)], identity[:])
+        bias = keep.tile([P, N // P, E], F32, name="bias")
+        nc.scalar.copy(bias[:], back[:, :, 0:E])
+        gate_t = keep.tile([P, T], F32, name="gate_t")
+        for h in range(2):
+            nc.scalar.copy(
+                gate_t[:].rearrange("p (k r) -> p k r", r=E)[:, :, 4 * h : 4 * h + 4], spread[h][:].rearrange("p r k -> p k r")
+            )
+
+        windows = [keep.tile([P, T], F32, name="window%d" % g) for g in range(N // P)]
 
         def group_of(groups, e):
             return [n for n, (e0, count) in enumerate(groups) if e0 <= e < e0 + count][0]
+
+        def shared(n, owned):
+            rows = STEPS[n][0]
+            return rows[0::2] if owned == "vector" else rows[1::2]
 
         def products(n, rows):
             experts = STEPS[n][1]
@@ -179,87 +203,80 @@ def tile_moe_two_lin_relu2_kernel(tc, xT, w_words, w_scales, b, gate, offs, dst,
             return bank
 
         def gate_of(experts):
-            s = group_of(SCALE_GROUPS, experts.start)
-            first = C * (experts.start - SCALE_GROUPS[s][0])
-            return gate_t[s][:, first : first + C * len(experts)]
+            return gate_t[:, C * experts.start : C * experts.stop]
 
-        def relu_on_scalar(r, n, rows):
+        def gate_over(n, rows):
+            experts = STEPS[n][1]
+            return gate_of(experts).unsqueeze(1).to_broadcast([P, len(rows), C * len(experts)])
+
+        def relu_on_scalar(n, rows, name):
+            experts = STEPS[n][1]
             bank = products(n, rows)
+            r = work.tile([P, len(rows), C * len(experts)], F32, name=name)
             for u, g in enumerate(rows):
-                for v, e in enumerate(STEPS[n][1]):
+                for v, e in enumerate(experts):
                     nc.scalar.activation(r[:, u, C * v : C * (v + 1)], bank[:, u, v, :], RELU, bias=bias[:, g, e : e + 1])
+            return r
 
-        def scatter_on_vector(g, experts, sq):
-            places = entries(dst_t, experts.start, len(experts))
-            nc.vector.tensor_tensor(windows[g][:].indirect(places), sq, gate_of(experts), MULT)
+        def begin(n):
+            experts = STEPS[n][1]
+            mine, theirs = shared(n, "vector"), shared(n, "scalar")
+            if n < SCALAR_STEPS:
+                pre = relu_on_scalar(n, theirs, "pre")
+                return relu_on_scalar(n, mine, "r"), pre
+            r = relu_on_scalar(n, mine, "r") if mine else None
+            bank = products(n, theirs)
+            pre = work.tile([P, len(theirs), C * len(experts)], F32, name="pre")
+            nc.vector.tensor_tensor(
+                pre[:].rearrange("p u (v c) -> p u v c", c=C),
+                bank[:],
+                bias[:, theirs.start : theirs.stop : theirs.step, experts.start : experts.stop]
+                .unsqueeze(3)
+                .to_broadcast([P, len(theirs), len(experts), C]),
+                ADD,
+            )
+            return r, pre
 
-        def scatter_on_scalar(g, experts, gated):
-            places = entries(dst_t, experts.start, len(experts))
-            nc.scalar.activation(windows[g][:].indirect(places), gated, COPY)
+        def clip(n, pre):
+            if n < SCALAR_STEPS or pre is None:
+                return None
+            clipped = work.tile(list(pre.shape), F32, name="clipped")
+            nc.vector.scalar_tensor_tensor(clipped[:], pre[:], 0.0, gate_over(n, shared(n, "scalar")), MAX, MULT)
+            return clipped
 
-        def spare(g, rows, width):
-            return windows[g][:, T : T + rows * width].rearrange("p (u c) -> p u c", c=width)
-
-        waiting = None
-        for n in range(WHOLE_STEPS):
-            rows, experts = STEPS[n]
-            second = n % 2
-            if not second:
-                sq = keep.tile([P, 4, 2 * C], F32, name="sq%d" % n)
-            if waiting:
-                r = spare(3, 4, C)
+        def finish(n, r, pre, clipped):
+            mine, theirs = shared(n, "vector"), shared(n, "scalar")
+            width = C * len(STEPS[n][1])
+            tag = "w%d" % (n + 1) if n in HELD else "ready%d" % n
+            ready = keep.tile([P, len(mine) + 2 * len(theirs), width], F32, name="ready%d" % n, tag=tag, align_bytes=64)
+            sq, gated = ready[:, 0 : len(mine), :], ready[:, len(mine) : len(mine) + len(theirs), :]
+            if n < SCALAR_STEPS:
+                ungated = ready[:, len(mine) + len(theirs) :, :]
+                nc.scalar.activation(ungated, pre[:], SQUARE)
+                nc.vector.tensor_tensor(gated, ungated, gate_over(n, theirs), MULT)
             else:
-                r = work.tile([P, 4, C], F32, name="r")[:, :, :]
-            relu_on_scalar(r[:, 0:2], n, rows[0:2])
-            relu_on_scalar(r[:, 2:4], n, rows[2:4])
-            mine = sq[:, :, C * second : C * (second + 1)]
-            nc.scalar.activation(mine, r, SQUARE)
-            if waiting:
-                scatter_on_scalar(3, *waiting)
-                waiting = None
-            if second:
-                pair = range(n - 1, n + 1)
-                gated = keep.tile([P, 2 * C], F32, name="gated%d" % n)
-                nc.vector.tensor_tensor(gated[:], sq[:, 3, :], gate_of(pair), MULT)
-                waiting = (pair, gated[:])
-            for g in rows[:-1]:
-                scatter_on_vector(g, experts, mine[:, g, :])
-        scatter_on_scalar(3, *waiting)
+                nc.vector.tensor_tensor(gated, clipped[:], pre[:], MULT)
+            if mine:
+                nc.scalar.activation(sq, r[:], SQUARE)
+            return sq, gated
 
-        def store(g):
-            nc.sync.dma_start(out=out[P * g : P * (g + 1), :], in_=windows[g][:, 0:T])
+        def scatter(n, sq, gated):
+            experts = STEPS[n][1]
+            places = entries(dst_t, experts.start, len(experts))
+            for u, g in enumerate(shared(n, "vector")):
+                nc.vector.tensor_tensor(windows[g][:].indirect(places), sq[:, u, :], gate_of(experts), MULT)
+            for u, g in enumerate(shared(n, "scalar")):
+                nc.scalar.activation(windows[g][:].indirect(places), gated[:, u, :], COPY)
+            if experts.stop == E:
+                for g in STEPS[n][0]:
+                    nc.sync.dma_start(out=out[P * g : P * (g + 1), :], in_=windows[g][:])
 
-        experts = STEPS[WHOLE_STEPS][1]
-        width = C * len(experts)
-        r = keep.tile([P, 2, width], F32, name="r_lower")
-        relu_on_scalar(r[:, 0:1], WHOLE_STEPS, range(0, 1))
-        relu_on_scalar(r[:, 1:2], WHOLE_STEPS, range(1, 2))
-        sq = keep.tile([P, 2, width], F32, name="sq_lower")
-        nc.scalar.activation(sq[:], r[:], SQUARE)
-        gated = keep.tile([P, width], F32, name="gated_lower")
-        nc.vector.tensor_tensor(gated[:], sq[:, 1, :], gate_of(experts), MULT)
-        scatter_on_vector(0, experts, sq[:, 0, :])
-        scatter_on_scalar(1, experts, gated[:])
-        store(0)
-        store(1)
-
-        bank = products(WHOLE_STEPS + 1, range(3, 4))
-        pre = keep.tile([P, width], F32, name="pre")
-        nc.vector.tensor_tensor(
-            pre[:].rearrange("p (v c) -> p v c", c=C),
-            bank[:, 0],
-            bias[:, 3, experts.start : experts.stop].unsqueeze(2).to_broadcast([P, len(experts), C]),
-            ADD,
-        )
-        clipped = keep.tile([P, width], F32, name="clipped")
-        nc.vector.scalar_tensor_tensor(clipped[:], pre[:], 0.0, gate_of(experts), MAX, MULT)
-        gated = keep.tile([P, width], F32, name="gated_upper")
-        nc.vector.tensor_tensor(gated[:], clipped[:], pre[:], MULT)
-        r = spare(3, 1, width)
-        relu_on_scalar(r, WHOLE_STEPS + 1, range(2, 3))
-        sq = keep.tile([P, width], F32, name="sq_upper")
-        nc.scalar.activation(sq[:], r[:, 0], SQUARE)
-        scatter_on_vector(2, experts, sq[:])
-        scatter_on_scalar(3, experts, gated[:])
-        store(2)
-        store(3)
+        r, pre = begin(0)
+        clipped = clip(0, pre)
+        for n in range(len(STEPS)):
+            last = n + 1 == len(STEPS)
+            next_r, next_pre = (None, None) if last else begin(n + 1)
+            sq, gated = finish(n, r, pre, clipped)
+            clipped = clip(n + 1, next_pre)
+            scatter(n, sq, gated)
+            r, pre = next_r, next_pre

@@ -26,9 +26,9 @@ PASSES = K // 512
 
 LOADS = ((512, 256, 256), (320, 384, 320), (384, 384, 256))
 QUANTS = ((256, 256, 256, 256), (512, 512), (512, 256, 256))
-VECTOR_COLUMNS = (((0, 256), (512, 640), (896, 1024)), ((832, 1024),), ((704, 768), (864, 1024)))
+VECTOR_COLUMNS = (((0, 256), (512, 640), (896, 1024)), ((896, 1024),), ((864, 1024),))
 GATHERS = [(0, 2), (2, 6)]
-SCALE_GROUPS = [(0, 2), (2, 2), (4, 2), (6, 2)]
+TOKEN_SCALES = ((0, 0), (1, 8), (1, 0))
 STEPS = [(range(4), range(e, e + 1)) for e in range(E - 2)] + [(range(2 * q, 2 * q + 2), range(E - 2, E)) for q in range(2)]
 SCALAR_STEPS = 1
 HELD = range(1, 7)
@@ -51,21 +51,30 @@ def tile_moe_two_lin_relu2_kernel(tc, xT, w_words, w_scales, b, gate, offs, dst,
         dst_t = lists.tile([P, T // 16], U16, name="dst_t")
 
         w_sc = []
-        for n, (e0, count) in enumerate(SCALE_GROUPS):
-            plane = keep.tile([P, count * PASSES, N], U8, name="w_sc%d" % n, align_bytes=64)
-            nc.vector.memset(plane[:].rearrange("p j n -> p (j n)").bitcast(I32), 0)
-            w_sc.append(plane)
-        x_sc = keep.tile([P, T], U8, name="x_sc", align_bytes=64)
-        nc.vector.memset(x_sc[:].bitcast(I32), 0)
+        for n in range(6):
+            block = keep.tile([P, N], U8, name="w_sc%d" % n, align_bytes=64)
+            nc.vector.memset(block[:].bitcast(I32), 0)
+            w_sc.append(block)
+        x_sc = []
+        for n in range(2):
+            plane = keep.tile([P, T], U8, name="x_sc%d" % n, align_bytes=64)
+            nc.vector.memset(plane[:].bitcast(I32), 0)
+            x_sc.append(plane)
 
-        sc_view = w_scales.rearrange("e a (q i) n -> i q (e a) n", i=4)
+        sc_view = w_scales.rearrange("(pair e) a q n -> pair (e a) q n", e=2)
+
+        def scale_home(e, a):
+            pair, place = e // 2, PASSES * (e % 2) + a
+            if place in (0, 5):
+                return 4 + place // 5, 4 * pair
+            return pair, 4 * (place - 1)
 
         def load_scales(n):
-            e0, count = SCALE_GROUPS[n]
-            for i in range(4):
+            planes = sc_view[n, 1:5] if n < 4 else sc_view[:, 5 * (n - 4)]
+            for quadrant in range(4):
                 nc.sync.dma_start(
-                    out=w_sc[n][i:P:32, :, :].bitcast(I32),
-                    in_=sc_view[i, :, PASSES * e0 : PASSES * (e0 + count), :].bitcast(I32),
+                    out=w_sc[n][32 * quadrant : 32 * quadrant + 16, :].bitcast(I32),
+                    in_=planes[:, 4 * quadrant : 4 * quadrant + 4, :].bitcast(I32),
                 )
 
         x_view = xT.rearrange("(a p j) w -> a p j w", p=P, j=4)
@@ -88,6 +97,7 @@ def tile_moe_two_lin_relu2_kernel(tc, xT, w_words, w_scales, b, gate, offs, dst,
             nc.sync.dma_start(out=wt[:].bitcast(I32), in_=source.bitcast(I32))
             w_tiles.append(wt)
 
+        load_scales(4)
         identity = keep.tile([P, P], F32, name="identity")
         make_identity(nc, identity[:])
         gate_rows = keep.tile([P, E], F32, name="gate_rows")
@@ -96,13 +106,14 @@ def tile_moe_two_lin_relu2_kernel(tc, xT, w_words, w_scales, b, gate, offs, dst,
         nc.gpsimd.memset(bias_rows[:, 4 * E :], 0.0)
         nc.sync.dma_start(out=bias_rows[:, 0 : 4 * E], in_=b.rearrange("(p j) e -> p (j e)", j=4))
 
-        for n, (e0, count) in enumerate(SCALE_GROUPS):
-            load_words(e0)
-            load_scales(n)
-            if n == 0:
+        for pair in range(E // 2):
+            load_words(2 * pair)
+            load_scales(pair)
+            if pair == 0:
                 nc.sync.dma_start(dst_t[:], dst)
-            for m in range(e0 + 1, e0 + count):
-                load_words(m)
+            load_words(2 * pair + 1)
+            if pair == 0:
+                load_scales(5)
 
         codes = [keep.tile([P, T], U32, name="codes%d" % a, align_bytes=64) for a in range(PASSES)]
         g_words = {}
@@ -110,7 +121,8 @@ def tile_moe_two_lin_relu2_kernel(tc, xT, w_words, w_scales, b, gate, offs, dst,
         for h, (e0, count) in enumerate(GATHERS):
             for a in range(PASSES):
                 g_words[h, a] = keep.tile([P, C * count], U32, name="gw%d_%d" % (h, a), align_bytes=64)
-            g_bytes[h] = keep.tile([P, C * count], U8, name="gb%d" % h, align_bytes=64)
+            for n in range(2):
+                g_bytes[h, n] = keep.tile([P, C * count], U8, name="gb%d_%d" % (h, n), align_bytes=64)
 
         def entries(tile, e0, count):
             return tile[:, C * e0 // 16 : C * (e0 + count) // 16]
@@ -118,8 +130,8 @@ def tile_moe_two_lin_relu2_kernel(tc, xT, w_words, w_scales, b, gate, offs, dst,
         def gather_words(a, h):
             nc.vector.tensor_copy(g_words[h, a][:], codes[a][:].indirect(entries(offs_t, *GATHERS[h])))
 
-        def gather_bytes(h):
-            nc.vector.tensor_copy(g_bytes[h][:], x_sc[:].indirect(entries(offs_t, *GATHERS[h])))
+        def gather_bytes(n, h):
+            nc.vector.tensor_copy(g_bytes[h, n][:], x_sc[n][:].indirect(entries(offs_t, *GATHERS[h])))
 
         for a in range(PASSES):
             starts = [lo for lo, hi in spans(LOADS[a])]
@@ -140,15 +152,18 @@ def tile_moe_two_lin_relu2_kernel(tc, xT, w_words, w_scales, b, gate, offs, dst,
                         )
                 nc.vector.quantize_mx(
                     out=codes[a][:, c0 : c0 + width].bitcast(FP8X4),
-                    scales=x_sc[4 * a : P, c0 : c0 + width],
+                    scales=x_sc[TOKEN_SCALES[a][0]][TOKEN_SCALES[a][1] : P, c0 : c0 + width],
                     in_=grouped[:].rearrange("p w j -> p (w j)"),
                 )
             if a < PASSES - 1:
                 for h in range(len(GATHERS)):
                     gather_words(a, h)
+            if a == 0:
+                for h in range(len(GATHERS)):
+                    gather_bytes(0, h)
         for h in range(len(GATHERS)):
             gather_words(PASSES - 1, h)
-            gather_bytes(h)
+            gather_bytes(1, h)
 
         turned = psum.tile([P, 4, P], F32, name="bank", bufs=8)
         for j in range(4):
@@ -187,16 +202,17 @@ def tile_moe_two_lin_relu2_kernel(tc, xT, w_words, w_scales, b, gate, offs, dst,
             for u, g in enumerate(rows):
                 for v, e in enumerate(experts):
                     h = group_of(GATHERS, e)
-                    s = group_of(SCALE_GROUPS, e)
                     slots = slice(C * (e - GATHERS[h][0]), C * (e + 1 - GATHERS[h][0]))
                     first = 512 * (g - STEPS[n][0].start)
                     for a in range(PASSES):
+                        block, start = scale_home(e, a)
+                        tile, token_start = TOKEN_SCALES[a]
                         nc.tensor.matmul_mx(
                             out=bank[:, u, v, :],
                             lhsT=w_tiles[n][:, PASSES * v + a, first : first + 512].bitcast(FP8X4),
-                            lhsT_scale=w_sc[s][:, PASSES * (e - SCALE_GROUPS[s][0]) + a, P * g : P * (g + 1)],
+                            lhsT_scale=w_sc[block][start:P, P * g : P * (g + 1)],
                             rhs=g_words[h, a][:, slots].bitcast(FP8X4),
-                            rhs_scale=g_bytes[h][4 * a : P, slots],
+                            rhs_scale=g_bytes[h, tile][token_start:P, slots],
                             start=(a == 0),
                             stop=(a == PASSES - 1),
                         )

@@ -31,7 +31,7 @@ GATHERS = [(0, 2), (2, 6)]
 TOKEN_SCALES = ((0, 0), (1, 8), (1, 0))
 STEPS = [(range(4), range(e, e + 1)) for e in range(E - 2)] + [(range(2 * q, 2 * q + 2), range(E - 2, E)) for q in range(2)]
 SCALAR_STEPS = 1
-HELD = range(1, 7)
+HELD = {"vector": range(0, 7), "scalar": range(2, 7)}
 
 
 def spans(widths):
@@ -221,78 +221,62 @@ def tile_moe_two_lin_relu2_kernel(tc, xT, w_words, w_scales, b, gate, offs, dst,
         def gate_of(experts):
             return gate_t[:, C * experts.start : C * experts.stop]
 
-        def gate_over(n, rows):
-            experts = STEPS[n][1]
-            return gate_of(experts).unsqueeze(1).to_broadcast([P, len(rows), C * len(experts)])
-
-        def relu_on_scalar(n, rows, name):
-            experts = STEPS[n][1]
+        def prepare(n, owned):
+            rows, experts = shared(n, owned), STEPS[n][1]
             bank = products(n, rows)
-            r = work.tile([P, len(rows), C * len(experts)], F32, name=name)
+            shape = [P, len(rows), C * len(experts)]
+            relu = work.tile(shape, F32, name="relu_" + owned)
+            other = work.tile(shape, F32, name="other_" + owned)
+            by_scalar = owned == "scalar" or n < SCALAR_STEPS
             for u, g in enumerate(rows):
                 for v, e in enumerate(experts):
-                    nc.scalar.activation(r[:, u, C * v : C * (v + 1)], bank[:, u, v, :], RELU, bias=bias[:, g, e : e + 1])
-            return r
+                    columns = slice(C * v, C * (v + 1))
+                    column = bias[:, g, e : e + 1]
+                    if by_scalar:
+                        nc.scalar.activation(relu[:, u, columns], bank[:, u, v, :], RELU, bias=column)
+                    else:
+                        nc.vector.tensor_scalar(relu[:, u, columns], bank[:, u, v, :], column, 0.0, ADD, MAX)
+                        nc.vector.scalar_tensor_tensor(
+                            other[:, u, columns], bank[:, u, v, :], column, gate_of(range(e, e + 1)), ADD, MULT
+                        )
+            if by_scalar:
+                nc.scalar.activation(other[:], relu[:], SQUARE)
+                return other[:], gate_of(experts).unsqueeze(1).to_broadcast(shape)
+            return other[:], relu[:]
 
-        def begin(n):
-            experts = STEPS[n][1]
-            mine, theirs = shared(n, "vector"), shared(n, "scalar")
-            if n < SCALAR_STEPS:
-                pre = relu_on_scalar(n, theirs, "pre")
-                return relu_on_scalar(n, mine, "r"), pre
-            r = relu_on_scalar(n, mine, "r") if mine else None
-            bank = products(n, theirs)
-            pre = work.tile([P, len(theirs), C * len(experts)], F32, name="pre")
-            nc.vector.tensor_tensor(
-                pre[:].rearrange("p u (v c) -> p u v c", c=C),
-                bank[:],
-                bias[:, theirs.start : theirs.stop : theirs.step, experts.start : experts.stop]
-                .unsqueeze(3)
-                .to_broadcast([P, len(theirs), len(experts), C]),
-                ADD,
-            )
-            return r, pre
-
-        def clip(n, pre):
-            if n < SCALAR_STEPS or pre is None:
-                return None
-            clipped = work.tile(list(pre.shape), F32, name="clipped")
-            nc.vector.scalar_tensor_tensor(clipped[:], pre[:], 0.0, gate_over(n, shared(n, "scalar")), MAX, MULT)
-            return clipped
-
-        def finish(n, r, pre, clipped):
-            mine, theirs = shared(n, "vector"), shared(n, "scalar")
+        def finish(n, factors):
             width = C * len(STEPS[n][1])
-            tag = "w%d" % (n + 1) if n in HELD else "ready%d" % n
-            ready = keep.tile([P, len(mine) + 2 * len(theirs), width], F32, name="ready%d" % n, tag=tag, align_bytes=64)
-            sq, gated = ready[:, 0 : len(mine), :], ready[:, len(mine) : len(mine) + len(theirs), :]
-            if n < SCALAR_STEPS:
-                ungated = ready[:, len(mine) + len(theirs) :, :]
-                nc.scalar.activation(ungated, pre[:], SQUARE)
-                nc.vector.tensor_tensor(gated, ungated, gate_over(n, theirs), MULT)
-            else:
-                nc.vector.tensor_tensor(gated, clipped[:], pre[:], MULT)
-            if mine:
-                nc.scalar.activation(sq, r[:], SQUARE)
-            return sq, gated
+            held = [owned for owned in factors if n in HELD[owned]]
+            ready = {}
+            if held:
+                both = keep.tile([P, len(STEPS[n][0]), width], F32, name="ready%d" % n, tag="w%d" % (n + 1), align_bytes=64)
+            for place, owned in enumerate(("vector", "scalar")):
+                count = len(shared(n, owned))
+                if owned in held:
+                    ready[owned] = both[:, place * count : (place + 1) * count, :]
+                else:
+                    free = keep.tile([P, count, width], F32, name="free%d_%s" % (n, owned))
+                    ready[owned] = free[:]
+                nc.gpsimd.tensor_tensor(ready[owned], factors[owned][0], factors[owned][1], MULT)
+            return ready
 
-        def scatter(n, sq, gated):
+        def scatter(n, ready):
             experts = STEPS[n][1]
             places = entries(dst_t, experts.start, len(experts))
             for u, g in enumerate(shared(n, "vector")):
-                nc.vector.tensor_tensor(windows[g][:].indirect(places), sq[:, u, :], gate_of(experts), MULT)
+                nc.vector.tensor_copy(windows[g][:].indirect(places), ready["vector"][:, u, :])
             for u, g in enumerate(shared(n, "scalar")):
-                nc.scalar.activation(windows[g][:].indirect(places), gated[:, u, :], COPY)
+                nc.scalar.activation(windows[g][:].indirect(places), ready["scalar"][:, u, :], COPY)
             if experts.stop == E:
                 for g in STEPS[n][0]:
                     nc.sync.dma_start(out=out[P * g : P * (g + 1), :], in_=windows[g][:])
 
-        r, pre = begin(0)
-        clipped = clip(0, pre)
+        def begin(n):
+            order = ("scalar", "vector") if n < SCALAR_STEPS else ("vector", "scalar")
+            return {owned: prepare(n, owned) for owned in order}
+
+        factors = begin(0)
         for n in range(len(STEPS)):
-            last = n + 1 == len(STEPS)
-            next_r, next_pre = (None, None) if last else begin(n + 1)
-            sq, gated = finish(n, r, pre, clipped)
-            clipped = clip(n + 1, next_pre)
-            scatter(n, sq, gated)
-            r, pre = next_r, next_pre
+            following = begin(n + 1) if n + 1 < len(STEPS) else None
+            scatter(n, finish(n, factors))
+            factors = following

@@ -26,12 +26,15 @@ PASSES = K // 512
 
 LOADS = ((512, 256, 256), (320, 384, 320), (384, 384, 256))
 QUANTS = ((256, 256, 256, 256), (512, 512), (512, 256, 256))
-VECTOR_COLUMNS = (((0, 256), (512, 640), (896, 1024)), ((896, 1024),), ((864, 1024),))
+VECTOR_COLUMNS = (((0, 256), (512, 640), (896, 1024)), ((832, 1024),), ((704, 768), (864, 1024)))
 GATHERS = [(0, 2), (2, 6)]
-TOKEN_SCALES = ((0, 0), (1, 8), (1, 0))
-STEPS = [(range(4), range(e, e + 1)) for e in range(E - 2)] + [(range(2 * q, 2 * q + 2), range(E - 2, E)) for q in range(2)]
-SCALAR_STEPS = 1
-HELD = {"vector": range(0, 7), "scalar": range(2, 7)}
+TOKEN_START = (0, 8, 12)
+RUNS = [range(first, first + 4) for left in range(0, E * PASSES, 9) for first in (left + 1, left + 5) if first + 4 <= E * PASSES]
+LEFT = [range(0, 10, 9), range(18, 24, 5)]
+STEPS = [(range(4), range(e, e + 1)) for e in range(E // 2)] + [
+    (range(2 * q, 2 * q + 2), range(e, e + 2)) for q in range(2) for e in range(E // 2, E, 2)
+]
+SPARE = 4 * C
 
 
 def spans(widths):
@@ -51,31 +54,28 @@ def tile_moe_two_lin_relu2_kernel(tc, xT, w_words, w_scales, b, gate, offs, dst,
         dst_t = lists.tile([P, T // 16], U16, name="dst_t")
 
         w_sc = []
-        for n in range(6):
+        for n in range(len(RUNS + LEFT)):
             block = keep.tile([P, N], U8, name="w_sc%d" % n, align_bytes=64)
             nc.vector.memset(block[:].bitcast(I32), 0)
             w_sc.append(block)
-        x_sc = []
-        for n in range(2):
-            plane = keep.tile([P, T], U8, name="x_sc%d" % n, align_bytes=64)
-            nc.vector.memset(plane[:].bitcast(I32), 0)
-            x_sc.append(plane)
+        x_sc = keep.tile([P, T], U8, name="x_sc", align_bytes=64)
+        nc.vector.memset(x_sc[:].bitcast(I32), 0)
 
-        sc_view = w_scales.rearrange("(pair e) a q n -> pair (e a) q n", e=2)
+        sc_view = w_scales.rearrange("e a q n -> (e a) q n")
+        loads = RUNS + LEFT
+        homes = {plane: (n, 4 * j) for n, planes in enumerate(loads) for j, plane in enumerate(planes)}
+        loaded = []
 
-        def scale_home(e, a):
-            pair, place = e // 2, PASSES * (e % 2) + a
-            if place in (0, 5):
-                return 4 + place // 5, 4 * pair
-            return pair, 4 * (place - 1)
-
-        def load_scales(n):
-            planes = sc_view[n, 1:5] if n < 4 else sc_view[:, 5 * (n - 4)]
-            for quadrant in range(4):
-                nc.sync.dma_start(
-                    out=w_sc[n][32 * quadrant : 32 * quadrant + 16, :].bitcast(I32),
-                    in_=planes[:, 4 * quadrant : 4 * quadrant + 4, :].bitcast(I32),
-                )
+        def load_scales(wanted):
+            for n, planes in enumerate(loads):
+                if planes not in loaded and any(plane in planes for plane in wanted):
+                    loaded.append(planes)
+                    for quadrant in range(4):
+                        first = 32 * quadrant
+                        nc.sync.dma_start(
+                            out=w_sc[n][first : first + 4 * len(planes), :].bitcast(I32),
+                            in_=sc_view[planes.start : planes.stop : planes.step, 4 * quadrant : 4 * quadrant + 4, :].bitcast(I32),
+                        )
 
         x_view = xT.rearrange("(a p j) w -> a p j w", p=P, j=4)
         raws = {}
@@ -97,7 +97,7 @@ def tile_moe_two_lin_relu2_kernel(tc, xT, w_words, w_scales, b, gate, offs, dst,
             nc.sync.dma_start(out=wt[:].bitcast(I32), in_=source.bitcast(I32))
             w_tiles.append(wt)
 
-        load_scales(4)
+        load_scales([0])
         identity = keep.tile([P, P], F32, name="identity")
         make_identity(nc, identity[:])
         gate_rows = keep.tile([P, E], F32, name="gate_rows")
@@ -106,14 +106,13 @@ def tile_moe_two_lin_relu2_kernel(tc, xT, w_words, w_scales, b, gate, offs, dst,
         nc.gpsimd.memset(bias_rows[:, 4 * E :], 0.0)
         nc.sync.dma_start(out=bias_rows[:, 0 : 4 * E], in_=b.rearrange("(p j) e -> p (j e)", j=4))
 
-        for pair in range(E // 2):
-            load_words(2 * pair)
-            load_scales(pair)
-            if pair == 0:
+        for n, (rows, experts) in enumerate(STEPS):
+            load_words(n)
+            load_scales(range(PASSES * experts.start, PASSES * experts.stop))
+            if n == 0:
                 nc.sync.dma_start(dst_t[:], dst)
-            load_words(2 * pair + 1)
-            if pair == 0:
-                load_scales(5)
+            if n == 2:
+                load_scales(LEFT[1][:1])
 
         codes = [keep.tile([P, T], U32, name="codes%d" % a, align_bytes=64) for a in range(PASSES)]
         g_words = {}
@@ -121,8 +120,7 @@ def tile_moe_two_lin_relu2_kernel(tc, xT, w_words, w_scales, b, gate, offs, dst,
         for h, (e0, count) in enumerate(GATHERS):
             for a in range(PASSES):
                 g_words[h, a] = keep.tile([P, C * count], U32, name="gw%d_%d" % (h, a), align_bytes=64)
-            for n in range(2):
-                g_bytes[h, n] = keep.tile([P, C * count], U8, name="gb%d_%d" % (h, n), align_bytes=64)
+            g_bytes[h] = keep.tile([P, C * count], U8, name="gb%d" % h, align_bytes=64)
 
         def entries(tile, e0, count):
             return tile[:, C * e0 // 16 : C * (e0 + count) // 16]
@@ -130,8 +128,8 @@ def tile_moe_two_lin_relu2_kernel(tc, xT, w_words, w_scales, b, gate, offs, dst,
         def gather_words(a, h):
             nc.vector.tensor_copy(g_words[h, a][:], codes[a][:].indirect(entries(offs_t, *GATHERS[h])))
 
-        def gather_bytes(n, h):
-            nc.vector.tensor_copy(g_bytes[h, n][:], x_sc[n][:].indirect(entries(offs_t, *GATHERS[h])))
+        def gather_bytes(h):
+            nc.vector.tensor_copy(g_bytes[h][:], x_sc[:].indirect(entries(offs_t, *GATHERS[h])))
 
         for a in range(PASSES):
             starts = [lo for lo, hi in spans(LOADS[a])]
@@ -152,18 +150,15 @@ def tile_moe_two_lin_relu2_kernel(tc, xT, w_words, w_scales, b, gate, offs, dst,
                         )
                 nc.vector.quantize_mx(
                     out=codes[a][:, c0 : c0 + width].bitcast(FP8X4),
-                    scales=x_sc[TOKEN_SCALES[a][0]][TOKEN_SCALES[a][1] : P, c0 : c0 + width],
+                    scales=x_sc[TOKEN_START[a] : P, c0 : c0 + width],
                     in_=grouped[:].rearrange("p w j -> p (w j)"),
                 )
             if a < PASSES - 1:
                 for h in range(len(GATHERS)):
                     gather_words(a, h)
-            if a == 0:
-                for h in range(len(GATHERS)):
-                    gather_bytes(0, h)
         for h in range(len(GATHERS)):
             gather_words(PASSES - 1, h)
-            gather_bytes(1, h)
+            gather_bytes(h)
 
         turned = psum.tile([P, 4, P], F32, name="bank", bufs=8)
         for j in range(4):
@@ -187,14 +182,10 @@ def tile_moe_two_lin_relu2_kernel(tc, xT, w_words, w_scales, b, gate, offs, dst,
                 gate_t[:].rearrange("p (k r) -> p k r", r=E)[:, :, 4 * h : 4 * h + 4], spread[h][:].rearrange("p r k -> p k r")
             )
 
-        windows = [keep.tile([P, T], F32, name="window%d" % g) for g in range(N // P)]
+        windows = [keep.tile([P, T + SPARE * (g == 3)], F32, name="window%d" % g) for g in range(N // P)]
 
         def group_of(groups, e):
             return [n for n, (e0, count) in enumerate(groups) if e0 <= e < e0 + count][0]
-
-        def shared(n, owned):
-            rows = STEPS[n][0]
-            return rows[0::2] if owned == "vector" else rows[1::2]
 
         def products(n, rows):
             experts = STEPS[n][1]
@@ -205,78 +196,73 @@ def tile_moe_two_lin_relu2_kernel(tc, xT, w_words, w_scales, b, gate, offs, dst,
                     slots = slice(C * (e - GATHERS[h][0]), C * (e + 1 - GATHERS[h][0]))
                     first = 512 * (g - STEPS[n][0].start)
                     for a in range(PASSES):
-                        block, start = scale_home(e, a)
-                        tile, token_start = TOKEN_SCALES[a]
+                        block, start = homes[PASSES * e + a]
                         nc.tensor.matmul_mx(
                             out=bank[:, u, v, :],
                             lhsT=w_tiles[n][:, PASSES * v + a, first : first + 512].bitcast(FP8X4),
                             lhsT_scale=w_sc[block][start:P, P * g : P * (g + 1)],
                             rhs=g_words[h, a][:, slots].bitcast(FP8X4),
-                            rhs_scale=g_bytes[h, tile][token_start:P, slots],
+                            rhs_scale=g_bytes[h][TOKEN_START[a] : P, slots],
                             start=(a == 0),
                             stop=(a == PASSES - 1),
                         )
             return bank
 
-        def gate_of(experts):
-            return gate_t[:, C * experts.start : C * experts.stop]
-
-        def prepare(n, owned):
-            rows, experts = shared(n, owned), STEPS[n][1]
-            bank = products(n, rows)
-            shape = [P, len(rows), C * len(experts)]
-            relu = work.tile(shape, F32, name="relu_" + owned)
-            other = work.tile(shape, F32, name="other_" + owned)
-            by_scalar = owned == "scalar" or n < SCALAR_STEPS
-            for u, g in enumerate(rows):
-                for v, e in enumerate(experts):
-                    columns = slice(C * v, C * (v + 1))
-                    column = bias[:, g, e : e + 1]
-                    if by_scalar:
-                        nc.scalar.activation(relu[:, u, columns], bank[:, u, v, :], RELU, bias=column)
-                    else:
-                        nc.vector.tensor_scalar(relu[:, u, columns], bank[:, u, v, :], column, 0.0, ADD, MAX)
-                        nc.vector.scalar_tensor_tensor(
-                            other[:, u, columns], bank[:, u, v, :], column, gate_of(range(e, e + 1)), ADD, MULT
-                        )
-            if by_scalar:
-                nc.scalar.activation(other[:], relu[:], SQUARE)
-                return other[:], gate_of(experts).unsqueeze(1).to_broadcast(shape)
-            return other[:], relu[:]
-
-        def finish(n, factors):
-            width = C * len(STEPS[n][1])
-            held = [owned for owned in factors if n in HELD[owned]]
-            ready = {}
-            if held:
-                both = keep.tile([P, len(STEPS[n][0]), width], F32, name="ready%d" % n, tag="w%d" % (n + 1), align_bytes=64)
-            for place, owned in enumerate(("vector", "scalar")):
-                count = len(shared(n, owned))
-                if owned in held:
-                    ready[owned] = both[:, place * count : (place + 1) * count, :]
-                else:
-                    free = keep.tile([P, count, width], F32, name="free%d_%s" % (n, owned))
-                    ready[owned] = free[:]
-                nc.gpsimd.tensor_tensor(ready[owned], factors[owned][0], factors[owned][1], MULT)
-            return ready
-
-        def scatter(n, ready):
+        def prepare(n, rows, ready, in_window):
             experts = STEPS[n][1]
-            places = entries(dst_t, experts.start, len(experts))
-            for u, g in enumerate(shared(n, "vector")):
-                nc.vector.tensor_copy(windows[g][:].indirect(places), ready["vector"][:, u, :])
-            for u, g in enumerate(shared(n, "scalar")):
-                nc.scalar.activation(windows[g][:].indirect(places), ready["scalar"][:, u, :], COPY)
-            if experts.stop == E:
-                for g in STEPS[n][0]:
-                    nc.sync.dma_start(out=out[P * g : P * (g + 1), :], in_=windows[g][:])
+            shape = [P, len(rows), C * len(experts)]
+            if in_window:
+                relu = windows[3][:, T:].rearrange("p (u c) -> p u c", u=len(rows))
+            else:
+                own = work.tile(shape, F32, name="relu")
+                relu = own[:]
+            square = work.tile(shape, F32, name="square")
+            half = len(rows) // 2
+            for u0 in (0, half):
+                bank = products(n, rows[u0 : u0 + half])
+                for u in range(half):
+                    for v, e in enumerate(experts):
+                        nc.scalar.activation(
+                            relu[:, u0 + u, C * v : C * (v + 1)], bank[:, u, v, :], RELU, bias=bias[:, rows[u0 + u], e : e + 1]
+                        )
+                if n == 0:
+                    nc.scalar.activation(square[:, u0 : u0 + half, :], relu[:, u0 : u0 + half, :], SQUARE)
+            if n > 0:
+                nc.scalar.activation(square[:], relu, SQUARE)
+            gates = gate_t[:, C * experts.start : C * experts.stop].unsqueeze(1).to_broadcast([P, half, shape[2]])
+            for u0 in (0, half):
+                nc.gpsimd.tensor_tensor(ready[:, u0 : u0 + half, :], square[:, u0 : u0 + half, :], gates, MULT)
 
-        def begin(n):
-            order = ("scalar", "vector") if n < SCALAR_STEPS else ("vector", "scalar")
-            return {owned: prepare(n, owned) for owned in order}
+        def on_vector(g, values, e0, count):
+            nc.vector.tensor_copy(windows[g][:].indirect(entries(dst_t, e0, count)), values)
 
-        factors = begin(0)
-        for n in range(len(STEPS)):
-            following = begin(n + 1) if n + 1 < len(STEPS) else None
-            scatter(n, finish(n, factors))
-            factors = following
+        def on_scalar(g, values, e0, count):
+            nc.scalar.activation(windows[g][:].indirect(entries(dst_t, e0, count)), values, COPY)
+
+        def store(g):
+            queue = nc.scalar if g == 3 else nc.sync
+            queue.dma_start(out=out[P * g : P * (g + 1), :], in_=windows[g][:, 0:T])
+
+        pairs = [keep.tile([P, N // P, 2 * C], F32, name="ready%d" % n) for n in range(E // 2)]
+        waiting = []
+        for n, (rows, experts) in enumerate(STEPS):
+            ready = pairs[experts.start // 2]
+            slots = slice(C * (experts.start % 2), C * (experts.start % 2 + len(experts)))
+            last = n + 1 == len(STEPS)
+            behind = len(waiting) > 0
+            prepare(n, rows, ready[:, rows.start : rows.stop, slots], behind)
+            if 3 in rows and experts.stop % 2 == 0 and last:
+                waiting.append(experts.stop - 2)
+            for g in rows:
+                if g != 3:
+                    on_vector(g, ready[:, g, slots], experts.start, len(experts))
+                    if experts.stop == E and not last:
+                        store(g)
+            if behind:
+                for e0 in waiting:
+                    on_scalar(3, pairs[e0 // 2][:, 3, :], e0, 2)
+                waiting = []
+            if 3 in rows and experts.stop % 2 == 0 and not last:
+                waiting.append(experts.stop - 2)
+        store(3)
+        store(2)

@@ -18,23 +18,30 @@ RELU = mybir.ActivationFunctionType.Relu
 SQUARE = mybir.ActivationFunctionType.Square
 COPY = mybir.ActivationFunctionType.Copy
 MULT = mybir.AluOpType.mult
-ADD = mybir.AluOpType.add
-MAX = mybir.AluOpType.max
 
 P = 128
 PASSES = K // 512
+BLOCKS = N // P
+WORD_BYTES = 4
 
 LOADS = ((512, 256, 256), (320, 384, 320), (384, 384, 256))
 QUANTS = ((256, 256, 256, 256), (512, 512), (512, 256, 256))
 VECTOR_COLUMNS = (((0, 256), (512, 640), (896, 1024)), ((832, 1024),), ((704, 768), (864, 1024)))
-GATHERS = [(0, 2), (2, 6)]
-TOKEN_START = (0, 8, 12)
-RUNS = [range(first, first + 4) for left in range(0, E * PASSES, 9) for first in (left + 1, left + 5) if first + 4 <= E * PASSES]
-LEFT = [range(0, 10, 9), range(18, 24, 5)]
-STEPS = [(range(4), range(e, e + 1)) for e in range(E // 2)] + [
-    (range(2 * q, 2 * q + 2), range(e, e + 2)) for q in range(2) for e in range(E // 2, E, 2)
+GATHERS = [range(0, 2), range(2, E)]
+
+TOKEN_START = (8, 12, 0)
+RUNS = [range(first, first + 4) for nine in range(0, E * PASSES, 9) for first in (nine, nine + 4) if first + 4 <= E * PASSES]
+LEFT_OVER = [range(8, 18, 9), range(22, 24)]
+PLANE_TILES = RUNS + LEFT_OVER
+
+STEPS = [(range(BLOCKS), range(e, e + 1)) for e in range(E // 2)] + [
+    (range(g, g + 2), range(e, e + 2)) for g in (0, 2) for e in range(E // 2, E, 2)
 ]
-SPARE = 4 * C
+LAST = len(STEPS) - 1
+SCALAR_BLOCK = 3
+SPARE = 2 * C
+WORK_BUFS = 4
+PSUM_BANKS = 8
 
 
 def spans(widths):
@@ -47,35 +54,19 @@ def tile_moe_two_lin_relu2_kernel(tc, xT, w_words, w_scales, b, gate, offs, dst,
     with ExitStack() as ctx:
         lists = ctx.enter_context(tc.tile_pool(name="lists", bufs=1))
         keep = ctx.enter_context(tc.tile_pool(name="keep", bufs=1))
-        work = ctx.enter_context(tc.tile_pool(name="work", bufs=4))
+        work = ctx.enter_context(tc.tile_pool(name="work", bufs=WORK_BUFS))
         psum = ctx.enter_context(tc.psum_pool(name="psum", bufs=1))
 
         offs_t = lists.tile([P, T // 16], U16, name="offs_t")
         dst_t = lists.tile([P, T // 16], U16, name="dst_t")
 
         w_sc = []
-        for n in range(len(RUNS + LEFT)):
-            block = keep.tile([P, N], U8, name="w_sc%d" % n, align_bytes=64)
-            nc.vector.memset(block[:].bitcast(I32), 0)
-            w_sc.append(block)
+        for n in range(len(PLANE_TILES)):
+            planes_tile = keep.tile([P, N], U8, name="w_sc%d" % n, align_bytes=64)
+            nc.vector.memset(planes_tile[:].bitcast(I32), 0)
+            w_sc.append(planes_tile)
         x_sc = keep.tile([P, T], U8, name="x_sc", align_bytes=64)
         nc.vector.memset(x_sc[:].bitcast(I32), 0)
-
-        sc_view = w_scales.rearrange("e a q n -> (e a) q n")
-        loads = RUNS + LEFT
-        homes = {plane: (n, 4 * j) for n, planes in enumerate(loads) for j, plane in enumerate(planes)}
-        loaded = []
-
-        def load_scales(wanted):
-            for n, planes in enumerate(loads):
-                if planes not in loaded and any(plane in planes for plane in wanted):
-                    loaded.append(planes)
-                    for quadrant in range(4):
-                        first = 32 * quadrant
-                        nc.sync.dma_start(
-                            out=w_sc[n][first : first + 4 * len(planes), :].bitcast(I32),
-                            in_=sc_view[planes.start : planes.stop : planes.step, 4 * quadrant : 4 * quadrant + 4, :].bitcast(I32),
-                        )
 
         x_view = xT.rearrange("(a p j) w -> a p j w", p=P, j=4)
         raws = {}
@@ -87,49 +78,55 @@ def tile_moe_two_lin_relu2_kernel(tc, xT, w_words, w_scales, b, gate, offs, dst,
             if a == 0:
                 nc.sync.dma_start(offs_t[:], offs)
 
-        w_view = w_words.rearrange("e a p n r -> p (e a) (n r)")
-        w_tiles = []
-
-        def load_words(n):
-            rows, experts = STEPS[n]
-            source = w_view[:, PASSES * experts.start : PASSES * experts.stop, 512 * rows.start : 512 * rows.stop]
-            wt = keep.tile(list(source.shape), U8, name="w%d" % n, tag="w%d" % n, align_bytes=64)
-            nc.sync.dma_start(out=wt[:].bitcast(I32), in_=source.bitcast(I32))
-            w_tiles.append(wt)
-
-        load_scales([0])
         identity = keep.tile([P, P], F32, name="identity")
         make_identity(nc, identity[:])
-        gate_rows = keep.tile([P, E], F32, name="gate_rows")
-        nc.sync.dma_start(out=gate_rows[:], in_=gate[0, :].rearrange("(k r) -> k r", r=E))
         bias_rows = keep.tile([P, 3 * E + P], F32, name="bias_rows")
         nc.gpsimd.memset(bias_rows[:, 4 * E :], 0.0)
         nc.sync.dma_start(out=bias_rows[:, 0 : 4 * E], in_=b.rearrange("(p j) e -> p (j e)", j=4))
+        gate_rows = keep.tile([P, E], F32, name="gate_rows")
+        nc.sync.dma_start(out=gate_rows[:], in_=gate[0, :].rearrange("(k r) -> k r", r=E))
 
+        sc_view = w_scales.rearrange("e a q n -> (e a) q n")
+        homes = {plane: (n, 4 * j) for n, planes in enumerate(PLANE_TILES) for j, plane in enumerate(planes)}
+        loaded = []
+
+        def load_scales(wanted):
+            for n, planes in enumerate(PLANE_TILES):
+                if planes not in loaded and any(plane in planes for plane in wanted):
+                    loaded.append(planes)
+                    for quadrant in range(4):
+                        nc.sync.dma_start(
+                            out=w_sc[n][32 * quadrant : 32 * quadrant + 4 * len(planes), :].bitcast(I32),
+                            in_=sc_view[planes.start : planes.stop : planes.step, 4 * quadrant : 4 * quadrant + 4, :].bitcast(I32),
+                        )
+
+        w_view = w_words.rearrange("e a p n r -> p (e a) (n r)")
+        block_bytes = P * WORD_BYTES
+        w_tiles = []
         for n, (rows, experts) in enumerate(STEPS):
-            load_words(n)
-            load_scales(range(PASSES * experts.start, PASSES * experts.stop))
+            wanted = range(PASSES * experts.start, PASSES * experts.stop)
+            load_scales(wanted[:4])
+            source = w_view[:, wanted.start : wanted.stop, block_bytes * rows.start : block_bytes * rows.stop]
+            words = keep.tile(list(source.shape), U8, name="w%d" % n, align_bytes=64)
+            nc.sync.dma_start(out=words[:].bitcast(I32), in_=source.bitcast(I32))
+            w_tiles.append(words)
+            load_scales(wanted)
             if n == 0:
                 nc.sync.dma_start(dst_t[:], dst)
-            if n == 2:
-                load_scales(LEFT[1][:1])
 
         codes = [keep.tile([P, T], U32, name="codes%d" % a, align_bytes=64) for a in range(PASSES)]
         g_words = {}
         g_bytes = {}
-        for h, (e0, count) in enumerate(GATHERS):
+        for h, experts in enumerate(GATHERS):
             for a in range(PASSES):
-                g_words[h, a] = keep.tile([P, C * count], U32, name="gw%d_%d" % (h, a), align_bytes=64)
-            g_bytes[h] = keep.tile([P, C * count], U8, name="gb%d" % h, align_bytes=64)
+                g_words[h, a] = keep.tile([P, C * len(experts)], U32, name="gw%d_%d" % (h, a), align_bytes=64)
+            g_bytes[h] = keep.tile([P, C * len(experts)], U8, name="gb%d" % h, align_bytes=64)
 
-        def entries(tile, e0, count):
-            return tile[:, C * e0 // 16 : C * (e0 + count) // 16]
+        def entries(list_tile, experts):
+            return list_tile[:, C * experts.start // 16 : C * experts.stop // 16]
 
         def gather_words(a, h):
-            nc.vector.tensor_copy(g_words[h, a][:], codes[a][:].indirect(entries(offs_t, *GATHERS[h])))
-
-        def gather_bytes(h):
-            nc.vector.tensor_copy(g_bytes[h][:], x_sc[:].indirect(entries(offs_t, *GATHERS[h])))
+            nc.vector.tensor_copy(g_words[h, a][:], codes[a][:].indirect(entries(offs_t, GATHERS[h])))
 
         for a in range(PASSES):
             starts = [lo for lo, hi in spans(LOADS[a])]
@@ -137,20 +134,19 @@ def tile_moe_two_lin_relu2_kernel(tc, xT, w_words, w_scales, b, gate, offs, dst,
                 set(starts + [T] + [lo for lo, hi in spans(QUANTS[a])] + [x for span in VECTOR_COLUMNS[a] for x in span])
             )
             for c0, c1 in spans(QUANTS[a]):
-                width = c1 - c0
-                grouped = keep.tile([P, width, 4], BF16, name="grouped%d_%d" % (a, c0), align_bytes=64)
+                grouped = keep.tile([P, c1 - c0, 4], BF16, name="grouped%d_%d" % (a, c0), align_bytes=64)
                 for x0, x1 in zip(cuts, cuts[1:]):
                     if c0 <= x0 < c1:
-                        on_vector = any(lo <= x0 < hi for lo, hi in VECTOR_COLUMNS[a])
-                        copy = nc.vector.tensor_copy if on_vector else nc.scalar.copy
+                        by_vector = any(lo <= x0 < hi for lo, hi in VECTOR_COLUMNS[a])
+                        copy = nc.vector.tensor_copy if by_vector else nc.scalar.copy
                         first = max(lo for lo in starts if lo <= x0)
                         copy(
                             grouped[:, x0 - c0 : x1 - c0, :].rearrange("p (c i) t -> p c t i", i=4),
                             raws[a, first][:, :, x0 - first : x1 - first].rearrange("p t (c i) -> p c t i", i=4),
                         )
                 nc.vector.quantize_mx(
-                    out=codes[a][:, c0 : c0 + width].bitcast(FP8X4),
-                    scales=x_sc[TOKEN_START[a] : P, c0 : c0 + width],
+                    out=codes[a][:, c0:c1].bitcast(FP8X4),
+                    scales=x_sc[TOKEN_START[a] : P, c0:c1],
                     in_=grouped[:].rearrange("p w j -> p (w j)"),
                 )
             if a < PASSES - 1:
@@ -158,23 +154,23 @@ def tile_moe_two_lin_relu2_kernel(tc, xT, w_words, w_scales, b, gate, offs, dst,
                     gather_words(a, h)
         for h in range(len(GATHERS)):
             gather_words(PASSES - 1, h)
-            gather_bytes(h)
+            nc.vector.tensor_copy(g_bytes[h][:], x_sc[:].indirect(entries(offs_t, GATHERS[h])))
 
-        turned = psum.tile([P, 4, P], F32, name="bank", bufs=8)
+        turned = psum.tile([P, 4, P], F32, name="bank", bufs=PSUM_BANKS)
         for j in range(4):
             nc.tensor.transpose(turned[:, j, :], bias_rows[:, E * j : E * j + P], identity[:])
         by_expert = keep.tile([P, P, 4], F32, name="by_expert")
         nc.scalar.copy(by_expert[:], turned[:].rearrange("e j p -> e p j"))
         spread = []
         for h in range(2):
-            half = psum.tile([P, 4, P], F32, name="bank", bufs=8)
+            four = psum.tile([P, 4, P], F32, name="bank", bufs=PSUM_BANKS)
             for r in range(4):
-                nc.tensor.transpose(half[:, r, :], gate_rows[:, 4 * h + r : 4 * h + r + 1].to_broadcast([P, P]), identity[:])
-            spread.append(half)
-        back = psum.tile([P, N // P, P], F32, name="bank", bufs=8)
-        for g in range(N // P):
+                nc.tensor.transpose(four[:, r, :], gate_rows[:, 4 * h + r : 4 * h + r + 1].to_broadcast([P, P]), identity[:])
+            spread.append(four)
+        back = psum.tile([P, BLOCKS, P], F32, name="bank", bufs=PSUM_BANKS)
+        for g in range(BLOCKS):
             nc.tensor.transpose(back[:, g, :], by_expert[:].rearrange("e p j -> e (p j)")[:, P * g : P * (g + 1)], identity[:])
-        bias = keep.tile([P, N // P, E], F32, name="bias")
+        bias = keep.tile([P, BLOCKS, E], F32, name="bias")
         nc.scalar.copy(bias[:], back[:, :, 0:E])
         gate_t = keep.tile([P, T], F32, name="gate_t")
         for h in range(2):
@@ -182,25 +178,22 @@ def tile_moe_two_lin_relu2_kernel(tc, xT, w_words, w_scales, b, gate, offs, dst,
                 gate_t[:].rearrange("p (k r) -> p k r", r=E)[:, :, 4 * h : 4 * h + 4], spread[h][:].rearrange("p r k -> p k r")
             )
 
-        windows = [keep.tile([P, T + SPARE * (g == 3)], F32, name="window%d" % g) for g in range(N // P)]
-
-        def group_of(groups, e):
-            return [n for n, (e0, count) in enumerate(groups) if e0 <= e < e0 + count][0]
+        windows = [keep.tile([P, T + SPARE * (g == SCALAR_BLOCK)], F32, name="window%d" % g) for g in range(BLOCKS)]
 
         def products(n, rows):
             experts = STEPS[n][1]
-            bank = psum.tile([P, len(rows), len(experts), C], F32, name="bank", bufs=8)
+            bank = psum.tile([P, len(rows), len(experts), C], F32, name="bank", bufs=PSUM_BANKS)
             for u, g in enumerate(rows):
                 for v, e in enumerate(experts):
-                    h = group_of(GATHERS, e)
-                    slots = slice(C * (e - GATHERS[h][0]), C * (e + 1 - GATHERS[h][0]))
-                    first = 512 * (g - STEPS[n][0].start)
+                    h = [e in gathered for gathered in GATHERS].index(True)
+                    slots = slice(C * (e - GATHERS[h].start), C * (e + 1 - GATHERS[h].start))
+                    first = block_bytes * (g - STEPS[n][0].start)
                     for a in range(PASSES):
-                        block, start = homes[PASSES * e + a]
+                        home, start = homes[PASSES * e + a]
                         nc.tensor.matmul_mx(
                             out=bank[:, u, v, :],
-                            lhsT=w_tiles[n][:, PASSES * v + a, first : first + 512].bitcast(FP8X4),
-                            lhsT_scale=w_sc[block][start:P, P * g : P * (g + 1)],
+                            lhsT=w_tiles[n][:, PASSES * v + a, first : first + block_bytes].bitcast(FP8X4),
+                            lhsT_scale=w_sc[home][start:P, P * g : P * (g + 1)],
                             rhs=g_words[h, a][:, slots].bitcast(FP8X4),
                             rhs_scale=g_bytes[h][TOKEN_START[a] : P, slots],
                             start=(a == 0),
@@ -208,61 +201,74 @@ def tile_moe_two_lin_relu2_kernel(tc, xT, w_words, w_scales, b, gate, offs, dst,
                         )
             return bank
 
-        def prepare(n, rows, ready, in_window):
-            experts = STEPS[n][1]
-            shape = [P, len(rows), C * len(experts)]
-            if in_window:
-                relu = windows[3][:, T:].rearrange("p (u c) -> p u c", u=len(rows))
-            else:
-                own = work.tile(shape, F32, name="relu")
-                relu = own[:]
-            square = work.tile(shape, F32, name="square")
+        def squares_of(n, in_window):
+            rows, experts = STEPS[n]
             half = len(rows) // 2
-            for u0 in (0, half):
-                bank = products(n, rows[u0 : u0 + half])
-                for u in range(half):
+            shape = [P, half, C * len(experts)]
+            second = work.tile(shape, F32, name="relu1")
+            if in_window:
+                relu = [windows[SCALAR_BLOCK][:, T:].rearrange("p (u c) -> p u c", u=half), second[:]]
+            else:
+                own = work.tile(shape, F32, name="relu0")
+                relu = [own[:], second[:]]
+            squares = [work.tile(shape, F32, name="square%d" % h) for h in range(2)]
+            for group in [rows[:half], rows[half:]] if n == 0 else [rows]:
+                bank = products(n, group)
+                for u, g in enumerate(group):
+                    h, place = divmod(g - rows.start, half)
                     for v, e in enumerate(experts):
                         nc.scalar.activation(
-                            relu[:, u0 + u, C * v : C * (v + 1)], bank[:, u, v, :], RELU, bias=bias[:, rows[u0 + u], e : e + 1]
+                            relu[h][:, place, C * v : C * (v + 1)], bank[:, u, v, :], RELU, bias=bias[:, g, e : e + 1]
                         )
-                if n == 0:
-                    nc.scalar.activation(square[:, u0 : u0 + half, :], relu[:, u0 : u0 + half, :], SQUARE)
-            if n > 0:
-                nc.scalar.activation(square[:], relu, SQUARE)
-            gates = gate_t[:, C * experts.start : C * experts.stop].unsqueeze(1).to_broadcast([P, half, shape[2]])
-            for u0 in (0, half):
-                nc.gpsimd.tensor_tensor(ready[:, u0 : u0 + half, :], square[:, u0 : u0 + half, :], gates, MULT)
+            for h in range(2):
+                nc.scalar.activation(squares[h][:], relu[h], SQUARE)
+            return squares
 
-        def on_vector(g, values, e0, count):
-            nc.vector.tensor_copy(windows[g][:].indirect(entries(dst_t, e0, count)), values)
+        def times_gate(n, values, squares):
+            experts = STEPS[n][1]
+            for h, square in enumerate(squares):
+                half = square.shape[1]
+                gates = gate_t[:, C * experts.start : C * experts.stop].unsqueeze(1).to_broadcast(list(square.shape))
+                nc.gpsimd.tensor_tensor(values[:, half * h : half * (h + 1), :], square[:], gates, MULT)
 
-        def on_scalar(g, values, e0, count):
-            nc.scalar.activation(windows[g][:].indirect(entries(dst_t, e0, count)), values, COPY)
+        def scatter_on_vector(g, values, experts):
+            nc.vector.tensor_copy(windows[g][:].indirect(entries(dst_t, experts)), values)
 
-        def store(g):
-            queue = nc.scalar if g == 3 else nc.sync
+        def scatter_on_scalar(g, values, experts):
+            nc.scalar.activation(windows[g][:].indirect(entries(dst_t, experts)), values, COPY)
+
+        def store(g, queue):
             queue.dma_start(out=out[P * g : P * (g + 1), :], in_=windows[g][:, 0:T])
 
-        pairs = [keep.tile([P, N // P, 2 * C], F32, name="ready%d" % n) for n in range(E // 2)]
-        waiting = []
-        for n, (rows, experts) in enumerate(STEPS):
-            ready = pairs[experts.start // 2]
-            slots = slice(C * (experts.start % 2), C * (experts.start % 2 + len(experts)))
-            last = n + 1 == len(STEPS)
-            behind = len(waiting) > 0
-            prepare(n, rows, ready[:, rows.start : rows.stop, slots], behind)
-            if 3 in rows and experts.stop % 2 == 0 and last:
-                waiting.append(experts.stop - 2)
-            for g in rows:
-                if g != 3:
-                    on_vector(g, ready[:, g, slots], experts.start, len(experts))
-                    if experts.stop == E and not last:
-                        store(g)
-            if behind:
-                for e0 in waiting:
-                    on_scalar(3, pairs[e0 // 2][:, 3, :], e0, 2)
-                waiting = []
-            if 3 in rows and experts.stop % 2 == 0 and not last:
-                waiting.append(experts.stop - 2)
-        store(3)
-        store(2)
+        gated = [keep.tile([P, BLOCKS, 2 * C], F32, name="gated%d" % i) for i in range(E // 2)]
+
+        def step_values(n):
+            rows, experts = STEPS[n]
+            first = C * (experts.start % 2)
+            return gated[experts.start // 2][:, rows.start : rows.stop, first : first + C * len(experts)]
+
+        for n in range(LAST - 1):
+            rows, experts = STEPS[n]
+            after_pair = n in (2, 4)
+            times_gate(n, step_values(n), squares_of(n, after_pair))
+            for u, g in enumerate(rows):
+                if g != SCALAR_BLOCK:
+                    scatter_on_vector(g, step_values(n)[:, u, :], experts)
+                    if experts.stop == E:
+                        store(g, nc.sync)
+            if after_pair:
+                scatter_on_scalar(SCALAR_BLOCK, gated[n // 2 - 1][:, SCALAR_BLOCK, :], range(n - 2, n))
+
+        rows, experts_before = STEPS[LAST - 1]
+        experts = STEPS[LAST][1]
+        squares_before = squares_of(LAST - 1, False)
+        squares = squares_of(LAST, True)
+        held = keep.tile([P, len(rows), 2 * C], F32, name="held", tag="w%d" % LAST, align_bytes=64)
+        times_gate(LAST - 1, held[:], squares_before)
+        times_gate(LAST, step_values(LAST), squares)
+        for u, g in enumerate(rows):
+            scatter_on_scalar(g, held[:, u, :], experts_before)
+        scatter_on_vector(rows[0], step_values(LAST)[:, 0, :], experts)
+        store(rows[0], nc.sync)
+        scatter_on_scalar(SCALAR_BLOCK, step_values(LAST)[:, 1, :], experts)
+        store(SCALAR_BLOCK, nc.scalar)

@@ -22,24 +22,29 @@ MULT = mybir.AluOpType.mult
 P = 128
 PASSES = K // 512
 BLOCKS = N // P
-WORD_BYTES = 4
+BLOCK_BYTES = 4 * P
 
-LOADS = ((512, 256, 256), (320, 384, 320), (384, 384, 256))
-QUANTS = ((256, 256, 256, 256), (512, 512), (512, 256, 256))
-VECTOR_COLUMNS = (((0, 256), (512, 640), (896, 1024)), ((832, 1024),), ((704, 768), (864, 1024)))
-GATHERS = [range(0, 2), range(2, E)]
+LOADS = ((1024,), (512,512), (512, 512))
+QUANTS = ((512, 512), (512, 512), (512, 256, 256))
+VECTOR_COLUMNS = (((0, 640),), ((832, 1024),), ((832, 1024),))
+EARLY_GATHERS = [range(0, 2), range(2, E)]
+LATE_GATHERS = [range(0, 1), range(1, 2), range(2, 5), range(5, E)]
 
 TOKEN_START = (8, 12, 0)
 RUNS = [range(first, first + 4) for nine in range(0, E * PASSES, 9) for first in (nine, nine + 4) if first + 4 <= E * PASSES]
 LEFT_OVER = [range(8, 18, 9), range(22, 24)]
-PLANE_TILES = RUNS + LEFT_OVER
+PLANE_TILES = sorted(RUNS + LEFT_OVER, key=lambda planes: planes.start)
 
-STEPS = [(range(BLOCKS), range(e, e + 1)) for e in range(E // 2)] + [
-    (range(g, g + 2), range(e, e + 2)) for g in (0, 2) for e in range(E // 2, E, 2)
+WHOLE = E // 2
+STEPS = [(range(BLOCKS), range(e, e + 1)) for e in range(WHOLE)] + [
+    (range(g, g + 2), range(e, e + 2)) for g in (0, 2) for e in range(WHOLE, E, 2)
 ]
 LAST = len(STEPS) - 1
-SCALAR_BLOCK = 3
-SPARE = 2 * C
+BEHIND = {3: (3, range(0, 2)), 4: (3, range(2, 4)), 5: (1, range(4, 6)), 6: (1, range(6, 8)), 7: (3, range(4, 6))}
+SPARE = 8
+POOL_SQUARES = (3, 4, 5, 6)
+UPPER_FIRST = ()
+TWO_BANKS = (0, 1, 2)
 WORK_BUFS = 4
 PSUM_BANKS = 8
 
@@ -68,6 +73,12 @@ def tile_moe_two_lin_relu2_kernel(tc, xT, w_words, w_scales, b, gate, offs, dst,
         x_sc = keep.tile([P, T], U8, name="x_sc", align_bytes=64)
         nc.vector.memset(x_sc[:].bitcast(I32), 0)
 
+        identity = keep.tile([P, P], F32, name="identity")
+        make_identity(nc, identity[:])
+        bias_rows = keep.tile([P, 3 * E + P], F32, name="bias_rows")
+        nc.gpsimd.memset(bias_rows[:, 4 * E :], 0.0)
+        gate_rows = keep.tile([P, E], F32, name="gate_rows")
+
         x_view = xT.rearrange("(a p j) w -> a p j w", p=P, j=4)
         raws = {}
         for a in range(PASSES):
@@ -77,56 +88,42 @@ def tile_moe_two_lin_relu2_kernel(tc, xT, w_words, w_scales, b, gate, offs, dst,
                 raws[a, lo] = raw
             if a == 0:
                 nc.sync.dma_start(offs_t[:], offs)
-
-        identity = keep.tile([P, P], F32, name="identity")
-        make_identity(nc, identity[:])
-        bias_rows = keep.tile([P, 3 * E + P], F32, name="bias_rows")
-        nc.gpsimd.memset(bias_rows[:, 4 * E :], 0.0)
         nc.sync.dma_start(out=bias_rows[:, 0 : 4 * E], in_=b.rearrange("(p j) e -> p (j e)", j=4))
-        gate_rows = keep.tile([P, E], F32, name="gate_rows")
         nc.sync.dma_start(out=gate_rows[:], in_=gate[0, :].rearrange("(k r) -> k r", r=E))
 
         sc_view = w_scales.rearrange("e a q n -> (e a) q n")
         homes = {plane: (n, 4 * j) for n, planes in enumerate(PLANE_TILES) for j, plane in enumerate(planes)}
-        loaded = []
-
-        def load_scales(wanted):
-            for n, planes in enumerate(PLANE_TILES):
-                if planes not in loaded and any(plane in planes for plane in wanted):
-                    loaded.append(planes)
-                    for quadrant in range(4):
-                        nc.sync.dma_start(
-                            out=w_sc[n][32 * quadrant : 32 * quadrant + 4 * len(planes), :].bitcast(I32),
-                            in_=sc_view[planes.start : planes.stop : planes.step, 4 * quadrant : 4 * quadrant + 4, :].bitcast(I32),
-                        )
-
         w_view = w_words.rearrange("e a p n r -> p (e a) (n r)")
-        block_bytes = P * WORD_BYTES
         w_tiles = []
         for n, (rows, experts) in enumerate(STEPS):
-            wanted = range(PASSES * experts.start, PASSES * experts.stop)
-            load_scales(wanted[:4])
-            source = w_view[:, wanted.start : wanted.stop, block_bytes * rows.start : block_bytes * rows.stop]
+            if n < len(PLANE_TILES):
+                planes = PLANE_TILES[n]
+                for quadrant in range(4):
+                    nc.sync.dma_start(
+                        out=w_sc[n][32 * quadrant : 32 * quadrant + 4 * len(planes), :].bitcast(I32),
+                        in_=sc_view[planes.start : planes.stop : planes.step, 4 * quadrant : 4 * quadrant + 4, :].bitcast(I32),
+                    )
+            source = w_view[
+                :, PASSES * experts.start : PASSES * experts.stop, BLOCK_BYTES * rows.start : BLOCK_BYTES * rows.stop
+            ]
             words = keep.tile(list(source.shape), U8, name="w%d" % n, align_bytes=64)
             nc.sync.dma_start(out=words[:].bitcast(I32), in_=source.bitcast(I32))
             w_tiles.append(words)
-            load_scales(wanted)
             if n == 0:
                 nc.sync.dma_start(dst_t[:], dst)
 
         codes = [keep.tile([P, T], U32, name="codes%d" % a, align_bytes=64) for a in range(PASSES)]
-        g_words = {}
-        g_bytes = {}
-        for h, experts in enumerate(GATHERS):
-            for a in range(PASSES):
-                g_words[h, a] = keep.tile([P, C * len(experts)], U32, name="gw%d_%d" % (h, a), align_bytes=64)
-            g_bytes[h] = keep.tile([P, C * len(experts)], U8, name="gb%d" % h, align_bytes=64)
+        g_words = [keep.tile([P, T], U32, name="g_words%d" % a, align_bytes=64) for a in range(PASSES)]
+        g_bytes = keep.tile([P, T], U8, name="g_bytes", align_bytes=64)
+
+        def slots(experts):
+            return slice(C * experts.start, C * experts.stop)
 
         def entries(list_tile, experts):
             return list_tile[:, C * experts.start // 16 : C * experts.stop // 16]
 
-        def gather_words(a, h):
-            nc.vector.tensor_copy(g_words[h, a][:], codes[a][:].indirect(entries(offs_t, GATHERS[h])))
+        def gather(gathered, window, experts):
+            nc.vector.tensor_copy(gathered[:, slots(experts)], window[:].indirect(entries(offs_t, experts)))
 
         for a in range(PASSES):
             starts = [lo for lo, hi in spans(LOADS[a])]
@@ -137,8 +134,8 @@ def tile_moe_two_lin_relu2_kernel(tc, xT, w_words, w_scales, b, gate, offs, dst,
                 grouped = keep.tile([P, c1 - c0, 4], BF16, name="grouped%d_%d" % (a, c0), align_bytes=64)
                 for x0, x1 in zip(cuts, cuts[1:]):
                     if c0 <= x0 < c1:
-                        by_vector = any(lo <= x0 < hi for lo, hi in VECTOR_COLUMNS[a])
-                        copy = nc.vector.tensor_copy if by_vector else nc.scalar.copy
+                        on_vector = any(lo <= x0 < hi for lo, hi in VECTOR_COLUMNS[a])
+                        copy = nc.vector.tensor_copy if on_vector else nc.scalar.copy
                         first = max(lo for lo in starts if lo <= x0)
                         copy(
                             grouped[:, x0 - c0 : x1 - c0, :].rearrange("p (c i) t -> p c t i", i=4),
@@ -150,11 +147,11 @@ def tile_moe_two_lin_relu2_kernel(tc, xT, w_words, w_scales, b, gate, offs, dst,
                     in_=grouped[:].rearrange("p w j -> p (w j)"),
                 )
             if a < PASSES - 1:
-                for h in range(len(GATHERS)):
-                    gather_words(a, h)
-        for h in range(len(GATHERS)):
-            gather_words(PASSES - 1, h)
-            nc.vector.tensor_copy(g_bytes[h][:], x_sc[:].indirect(entries(offs_t, GATHERS[h])))
+                for experts in EARLY_GATHERS:
+                    gather(g_words[a], codes[a], experts)
+        for experts in LATE_GATHERS:
+            gather(g_words[PASSES - 1], codes[PASSES - 1], experts)
+            gather(g_bytes, x_sc, experts)
 
         turned = psum.tile([P, 4, P], F32, name="bank", bufs=PSUM_BANKS)
         for j in range(4):
@@ -178,97 +175,91 @@ def tile_moe_two_lin_relu2_kernel(tc, xT, w_words, w_scales, b, gate, offs, dst,
                 gate_t[:].rearrange("p (k r) -> p k r", r=E)[:, :, 4 * h : 4 * h + 4], spread[h][:].rearrange("p r k -> p k r")
             )
 
-        windows = [keep.tile([P, T + SPARE * (g == SCALAR_BLOCK)], F32, name="window%d" % g) for g in range(BLOCKS)]
+        windows = [keep.tile([P, T + SPARE * (g % 2)], F32, name="window%d" % g) for g in range(BLOCKS)]
+        gated = [keep.tile([P, BLOCKS, 2 * C], F32, name="gated%d" % i) for i in range(E // 2)]
 
         def products(n, rows):
             experts = STEPS[n][1]
             bank = psum.tile([P, len(rows), len(experts), C], F32, name="bank", bufs=PSUM_BANKS)
             for u, g in enumerate(rows):
+                first = BLOCK_BYTES * (g - STEPS[n][0].start)
                 for v, e in enumerate(experts):
-                    h = [e in gathered for gathered in GATHERS].index(True)
-                    slots = slice(C * (e - GATHERS[h].start), C * (e + 1 - GATHERS[h].start))
-                    first = block_bytes * (g - STEPS[n][0].start)
                     for a in range(PASSES):
                         home, start = homes[PASSES * e + a]
                         nc.tensor.matmul_mx(
                             out=bank[:, u, v, :],
-                            lhsT=w_tiles[n][:, PASSES * v + a, first : first + block_bytes].bitcast(FP8X4),
+                            lhsT=w_tiles[n][:, PASSES * v + a, first : first + BLOCK_BYTES].bitcast(FP8X4),
                             lhsT_scale=w_sc[home][start:P, P * g : P * (g + 1)],
-                            rhs=g_words[h, a][:, slots].bitcast(FP8X4),
-                            rhs_scale=g_bytes[h][TOKEN_START[a] : P, slots],
+                            rhs=g_words[a][:, C * e : C * (e + 1)].bitcast(FP8X4),
+                            rhs_scale=g_bytes[TOKEN_START[a] : P, C * e : C * (e + 1)],
                             start=(a == 0),
                             stop=(a == PASSES - 1),
                         )
             return bank
 
-        def squares_of(n, in_window):
-            rows, experts = STEPS[n]
+        def halves_of(n):
+            rows = STEPS[n][0]
             half = len(rows) // 2
-            shape = [P, half, C * len(experts)]
-            second = work.tile(shape, F32, name="relu1")
-            if in_window:
-                relu = [windows[SCALAR_BLOCK][:, T:].rearrange("p (u c) -> p u c", u=half), second[:]]
-            else:
-                own = work.tile(shape, F32, name="relu0")
-                relu = [own[:], second[:]]
-            squares = [work.tile(shape, F32, name="square%d" % h) for h in range(2)]
-            for group in [rows[:half], rows[half:]] if n == 0 else [rows]:
+            return [rows[half:], rows[:half]] if n in UPPER_FIRST else [rows[:half], rows[half:]]
+
+        last_bias = {}
+        for n, (g, scattered_experts) in BEHIND.items():
+            place = T + len([m for m in last_bias if BEHIND[m][0] == g])
+            last_bias[n] = windows[g][:, place : place + 1]
+            e = STEPS[n][1][-1]
+            nc.scalar.copy(last_bias[n], back[:, halves_of(n)[1][-1], e : e + 1])
+
+        def prepare(n):
+            rows, experts = STEPS[n]
+            halves = halves_of(n)
+            shape = [P, len(halves[0]), C * len(experts)]
+            relu = [work.tile(shape, F32, name="relu%d" % h) for h in range(2)]
+            in_order = list(halves[0]) + list(halves[1])
+            for group in halves if n in TWO_BANKS else [in_order]:
                 bank = products(n, group)
                 for u, g in enumerate(group):
-                    h, place = divmod(g - rows.start, half)
+                    h, place = divmod(in_order.index(g), shape[1])
                     for v, e in enumerate(experts):
+                        last = n in BEHIND and g == in_order[-1] and e == experts[-1]
                         nc.scalar.activation(
-                            relu[h][:, place, C * v : C * (v + 1)], bank[:, u, v, :], RELU, bias=bias[:, g, e : e + 1]
+                            relu[h][:, place, C * v : C * (v + 1)],
+                            bank[:, u, v, :],
+                            RELU,
+                            bias=last_bias[n] if last else bias[:, g, e : e + 1],
                         )
-            for h in range(2):
-                nc.scalar.activation(squares[h][:], relu[h], SQUARE)
-            return squares
-
-        def times_gate(n, values, squares):
-            experts = STEPS[n][1]
-            for h, square in enumerate(squares):
-                half = square.shape[1]
-                gates = gate_t[:, C * experts.start : C * experts.stop].unsqueeze(1).to_broadcast(list(square.shape))
-                nc.gpsimd.tensor_tensor(values[:, half * h : half * (h + 1), :], square[:], gates, MULT)
-
-        def scatter_on_vector(g, values, experts):
-            nc.vector.tensor_copy(windows[g][:].indirect(entries(dst_t, experts)), values)
-
-        def scatter_on_scalar(g, values, experts):
-            nc.scalar.activation(windows[g][:].indirect(entries(dst_t, experts)), values, COPY)
-
-        def store(g, queue):
-            queue.dma_start(out=out[P * g : P * (g + 1), :], in_=windows[g][:, 0:T])
-
-        gated = [keep.tile([P, BLOCKS, 2 * C], F32, name="gated%d" % i) for i in range(E // 2)]
-
-        def step_values(n):
-            rows, experts = STEPS[n]
+            gates = gate_t[:, slots(experts)].unsqueeze(1).to_broadcast(shape)
             first = C * (experts.start % 2)
-            return gated[experts.start // 2][:, rows.start : rows.stop, first : first + C * len(experts)]
+            values = [gated[experts.start // 2][:, h.start : h.stop, first : first + C * len(experts)] for h in halves]
+            factors = [work.tile(shape, F32, name="factor%d" % h) for h in range(2)]
+            nc.scalar.activation(factors[0][:], relu[0][:], SQUARE)
+            if n in POOL_SQUARES:
+                nc.gpsimd.tensor_tensor(factors[1][:], relu[1][:], gates, MULT)
+            else:
+                nc.scalar.activation(factors[1][:], relu[1][:], SQUARE)
+            nc.gpsimd.tensor_tensor(values[0], factors[0][:], gates, MULT)
+            nc.gpsimd.tensor_tensor(values[1], factors[1][:], relu[1][:] if n in POOL_SQUARES else gates, MULT)
 
-        for n in range(LAST - 1):
-            rows, experts = STEPS[n]
-            after_pair = n in (2, 4)
-            times_gate(n, step_values(n), squares_of(n, after_pair))
-            for u, g in enumerate(rows):
-                if g != SCALAR_BLOCK:
-                    scatter_on_vector(g, step_values(n)[:, u, :], experts)
-                    if experts.stop == E:
-                        store(g, nc.sync)
-            if after_pair:
-                scatter_on_scalar(SCALAR_BLOCK, gated[n // 2 - 1][:, SCALAR_BLOCK, :], range(n - 2, n))
+        scattered = {g: [] for g in range(BLOCKS)}
 
-        rows, experts_before = STEPS[LAST - 1]
-        experts = STEPS[LAST][1]
-        squares_before = squares_of(LAST - 1, False)
-        squares = squares_of(LAST, True)
-        held = keep.tile([P, len(rows), 2 * C], F32, name="held", tag="w%d" % LAST, align_bytes=64)
-        times_gate(LAST - 1, held[:], squares_before)
-        times_gate(LAST, step_values(LAST), squares)
-        for u, g in enumerate(rows):
-            scatter_on_scalar(g, held[:, u, :], experts_before)
-        scatter_on_vector(rows[0], step_values(LAST)[:, 0, :], experts)
-        store(rows[0], nc.sync)
-        scatter_on_scalar(SCALAR_BLOCK, step_values(LAST)[:, 1, :], experts)
-        store(SCALAR_BLOCK, nc.scalar)
+        def scatter(g, experts, by_scalar):
+            first = C * (experts.start % 2)
+            values = gated[experts.start // 2][:, g, first : first + C * len(experts)]
+            places = windows[g][:].indirect(entries(dst_t, experts))
+            if by_scalar:
+                nc.scalar.activation(places, values, COPY)
+            else:
+                nc.vector.tensor_copy(places, values)
+            scattered[g].extend(experts)
+            if len(scattered[g]) == E:
+                queue = nc.scalar if g == BLOCKS - 1 else nc.sync
+                queue.dma_start(out=out[P * g : P * (g + 1), :], in_=windows[g][:, 0:T])
+
+        for n, (rows, experts) in enumerate(STEPS):
+            prepare(n)
+            if n in BEHIND:
+                scatter(BEHIND[n][0], BEHIND[n][1], True)
+            if n < WHOLE and n % 2 == 1:
+                scatter(1, range(n - 1, n + 1), False)
+            for g in rows[::2]:
+                scatter(g, experts, False)
+        scatter(BLOCKS - 1, STEPS[LAST][1], True)

@@ -40,11 +40,19 @@ STEPS = [(range(BLOCKS), range(e, e + 1)) for e in range(WHOLE)] + [
     (range(g, g + 2), range(e, e + 2)) for g in (0, 2) for e in range(WHOLE, E, 2)
 ]
 LAST = len(STEPS) - 1
-BEHIND = {3: (3, range(0, 2)), 4: (3, range(2, 4)), 5: (1, range(4, 6)), 6: (1, range(6, 8)), 7: (3, range(4, 6))}
+SHARED = 192
+BEHIND = {
+    2: (1, range(0, SHARED)),
+    3: (3, range(0, 2 * C)),
+    4: (3, range(2 * C, 4 * C)),
+    5: (1, range(4 * C, 4 * C + 256)),
+    6: (1, range(T - 256, T)),
+    7: (3, range(4 * C, 6 * C)),
+}
 SPARE = 8
-POOL_SQUARES = (3, 4, 5, 6)
+POOL_SQUARES = range(2, LAST)
 UPPER_FIRST = ()
-TWO_BANKS = (0, 1, 2)
+TWO_BANKS = range(5)
 WORK_BUFS = 4
 PSUM_BANKS = 8
 
@@ -176,7 +184,7 @@ def tile_moe_two_lin_relu2_kernel(tc, xT, w_words, w_scales, b, gate, offs, dst,
             )
 
         windows = [keep.tile([P, T + SPARE * (g % 2)], F32, name="window%d" % g) for g in range(BLOCKS)]
-        gated = [keep.tile([P, BLOCKS, 2 * C], F32, name="gated%d" % i) for i in range(E // 2)]
+        gated = keep.tile([P, BLOCKS, T], F32, name="gated")
 
         def products(n, rows):
             experts = STEPS[n][1]
@@ -228,8 +236,7 @@ def tile_moe_two_lin_relu2_kernel(tc, xT, w_words, w_scales, b, gate, offs, dst,
                             bias=last_bias[n] if last else bias[:, g, e : e + 1],
                         )
             gates = gate_t[:, slots(experts)].unsqueeze(1).to_broadcast(shape)
-            first = C * (experts.start % 2)
-            values = [gated[experts.start // 2][:, h.start : h.stop, first : first + C * len(experts)] for h in halves]
+            values = [gated[:, h.start : h.stop, slots(experts)] for h in halves]
             factors = [work.tile(shape, F32, name="factor%d" % h) for h in range(2)]
             nc.scalar.activation(factors[0][:], relu[0][:], SQUARE)
             if n in POOL_SQUARES:
@@ -241,16 +248,15 @@ def tile_moe_two_lin_relu2_kernel(tc, xT, w_words, w_scales, b, gate, offs, dst,
 
         scattered = {g: [] for g in range(BLOCKS)}
 
-        def scatter(g, experts, by_scalar):
-            first = C * (experts.start % 2)
-            values = gated[experts.start // 2][:, g, first : first + C * len(experts)]
-            places = windows[g][:].indirect(entries(dst_t, experts))
+        def scatter(g, taken, by_scalar):
+            values = gated[:, g, taken.start : taken.stop]
+            places = windows[g][:].indirect(dst_t[:, taken.start // 16 : taken.stop // 16])
             if by_scalar:
                 nc.scalar.activation(places, values, COPY)
             else:
                 nc.vector.tensor_copy(places, values)
-            scattered[g].extend(experts)
-            if len(scattered[g]) == E:
+            scattered[g].extend(taken)
+            if len(scattered[g]) == T:
                 queue = nc.scalar if g == BLOCKS - 1 else nc.sync
                 queue.dma_start(out=out[P * g : P * (g + 1), :], in_=windows[g][:, 0:T])
 
@@ -258,8 +264,8 @@ def tile_moe_two_lin_relu2_kernel(tc, xT, w_words, w_scales, b, gate, offs, dst,
             prepare(n)
             if n in BEHIND:
                 scatter(BEHIND[n][0], BEHIND[n][1], True)
-            if n < WHOLE and n % 2 == 1:
-                scatter(1, range(n - 1, n + 1), False)
+            if n == WHOLE - 1:
+                scatter(1, range(SHARED, WHOLE * C), False)
             for g in rows[::2]:
-                scatter(g, experts, False)
-        scatter(BLOCKS - 1, STEPS[LAST][1], True)
+                scatter(g, range(C * experts.start, C * experts.stop), False)
+        scatter(BLOCKS - 1, range(6 * C, T), True)

@@ -24,9 +24,9 @@ PASSES = K // 512
 BLOCKS = N // P
 BLOCK_BYTES = 4 * P
 
-LOADS = ((1024,), (512,512), (512, 512))
-QUANTS = ((512, 512), (512, 512), (512, 256, 256))
-VECTOR_COLUMNS = (((0, 640),), ((832, 1024),), ((832, 1024),))
+LOADS = ((1024,), (512, 512), (512, 512))
+QUANTS = ((512, 256, 256), (512, 256, 256), (512, 256, 256))
+VECTOR_COLUMNS = (((0, 512),(896,1024)), ((832, 1024),), ((832, 1024),))
 EARLY_GATHERS = [range(0, 2), range(2, E)]
 LATE_GATHERS = [range(0, 1), range(1, 2), range(2, 5), range(5, E)]
 
@@ -40,19 +40,18 @@ STEPS = [(range(BLOCKS), range(e, e + 1)) for e in range(WHOLE)] + [
     (range(g, g + 2), range(e, e + 2)) for g in (0, 2) for e in range(WHOLE, E, 2)
 ]
 LAST = len(STEPS) - 1
-SHARED = 192
+SHARED = 256
 BEHIND = {
     2: (1, range(0, SHARED)),
     3: (3, range(0, 2 * C)),
     4: (3, range(2 * C, 4 * C)),
     5: (1, range(4 * C, 4 * C + 256)),
-    6: (1, range(T - 256, T)),
     7: (3, range(4 * C, 6 * C)),
 }
 SPARE = 8
-POOL_SQUARES = range(2, LAST)
-UPPER_FIRST = ()
-TWO_BANKS = range(5)
+POOL_SQUARES = range(2, 6)
+UPPER_FIRST = (6,)
+TWO_BANKS = range(len(STEPS))
 WORK_BUFS = 4
 PSUM_BANKS = 8
 
@@ -117,7 +116,7 @@ def tile_moe_two_lin_relu2_kernel(tc, xT, w_words, w_scales, b, gate, offs, dst,
             words = keep.tile(list(source.shape), U8, name="w%d" % n, align_bytes=64)
             nc.sync.dma_start(out=words[:].bitcast(I32), in_=source.bitcast(I32))
             w_tiles.append(words)
-            if n == 0:
+            if n == 2:
                 nc.sync.dma_start(dst_t[:], dst)
 
         codes = [keep.tile([P, T], U32, name="codes%d" % a, align_bytes=64) for a in range(PASSES)]
@@ -134,26 +133,27 @@ def tile_moe_two_lin_relu2_kernel(tc, xT, w_words, w_scales, b, gate, offs, dst,
             nc.vector.tensor_copy(gathered[:, slots(experts)], window[:].indirect(entries(offs_t, experts)))
 
         for a in range(PASSES):
-            starts = [lo for lo, hi in spans(LOADS[a])]
-            cuts = sorted(
-                set(starts + [T] + [lo for lo, hi in spans(QUANTS[a])] + [x for span in VECTOR_COLUMNS[a] for x in span])
-            )
-            for c0, c1 in spans(QUANTS[a]):
-                grouped = keep.tile([P, c1 - c0, 4], BF16, name="grouped%d_%d" % (a, c0), align_bytes=64)
+            grouped = {
+                c0: keep.tile([P, c1 - c0, 4], BF16, name="grouped%d_%d" % (a, c0), align_bytes=64) for c0, c1 in spans(QUANTS[a])
+            }
+            cuts = sorted(set([lo for lo, hi in spans(LOADS[a])] + [T] + list(grouped) + [x for span in VECTOR_COLUMNS[a] for x in span]))
+            for lo, hi in spans(LOADS[a]):
                 for x0, x1 in zip(cuts, cuts[1:]):
-                    if c0 <= x0 < c1:
-                        on_vector = any(lo <= x0 < hi for lo, hi in VECTOR_COLUMNS[a])
+                    if lo <= x0 < hi:
+                        on_vector = any(first <= x0 < last for first, last in VECTOR_COLUMNS[a])
                         copy = nc.vector.tensor_copy if on_vector else nc.scalar.copy
-                        first = max(lo for lo in starts if lo <= x0)
+                        c0 = max(c for c in grouped if c <= x0)
                         copy(
-                            grouped[:, x0 - c0 : x1 - c0, :].rearrange("p (c i) t -> p c t i", i=4),
-                            raws[a, first][:, :, x0 - first : x1 - first].rearrange("p t (c i) -> p c t i", i=4),
+                            grouped[c0][:, x0 - c0 : x1 - c0, :].rearrange("p (c i) t -> p c t i", i=4),
+                            raws[a, lo][:, :, x0 - lo : x1 - lo].rearrange("p t (c i) -> p c t i", i=4),
                         )
-                nc.vector.quantize_mx(
-                    out=codes[a][:, c0:c1].bitcast(FP8X4),
-                    scales=x_sc[TOKEN_START[a] : P, c0:c1],
-                    in_=grouped[:].rearrange("p w j -> p (w j)"),
-                )
+                for c0, c1 in spans(QUANTS[a]):
+                    if lo < c1 <= hi:
+                        nc.vector.quantize_mx(
+                            out=codes[a][:, c0:c1].bitcast(FP8X4),
+                            scales=x_sc[TOKEN_START[a] : P, c0:c1],
+                            in_=grouped[c0][:].rearrange("p w j -> p (w j)"),
+                        )
             if a < PASSES - 1:
                 for experts in EARLY_GATHERS:
                     gather(g_words[a], codes[a], experts)
@@ -175,13 +175,13 @@ def tile_moe_two_lin_relu2_kernel(tc, xT, w_words, w_scales, b, gate, offs, dst,
         back = psum.tile([P, BLOCKS, P], F32, name="bank", bufs=PSUM_BANKS)
         for g in range(BLOCKS):
             nc.tensor.transpose(back[:, g, :], by_expert[:].rearrange("e p j -> e (p j)")[:, P * g : P * (g + 1)], identity[:])
-        bias = keep.tile([P, BLOCKS, E], F32, name="bias")
-        nc.scalar.copy(bias[:], back[:, :, 0:E])
         gate_t = keep.tile([P, T], F32, name="gate_t")
         for h in range(2):
             nc.scalar.copy(
                 gate_t[:].rearrange("p (k r) -> p k r", r=E)[:, :, 4 * h : 4 * h + 4], spread[h][:].rearrange("p r k -> p k r")
             )
+        bias = keep.tile([P, BLOCKS, E], F32, name="bias")
+        nc.scalar.copy(bias[:], back[:, :, 0:E])
 
         windows = [keep.tile([P, T + SPARE * (g % 2)], F32, name="window%d" % g) for g in range(BLOCKS)]
         gated = keep.tile([P, BLOCKS, T], F32, name="gated")
@@ -223,7 +223,8 @@ def tile_moe_two_lin_relu2_kernel(tc, xT, w_words, w_scales, b, gate, offs, dst,
             shape = [P, len(halves[0]), C * len(experts)]
             relu = [work.tile(shape, F32, name="relu%d" % h) for h in range(2)]
             in_order = list(halves[0]) + list(halves[1])
-            for group in halves if n in TWO_BANKS else [in_order]:
+            groups = halves if n in TWO_BANKS else [in_order]
+            for group in [[g] for g in in_order] if n in range(WHOLE) else groups:
                 bank = products(n, group)
                 for u, g in enumerate(group):
                     h, place = divmod(in_order.index(g), shape[1])
@@ -266,6 +267,6 @@ def tile_moe_two_lin_relu2_kernel(tc, xT, w_words, w_scales, b, gate, offs, dst,
                 scatter(BEHIND[n][0], BEHIND[n][1], True)
             if n == WHOLE - 1:
                 scatter(1, range(SHARED, WHOLE * C), False)
-            for g in rows[::2]:
+            for g in rows if n == 5 else rows[::2]:
                 scatter(g, range(C * experts.start, C * experts.stop), False)
         scatter(BLOCKS - 1, range(6 * C, T), True)

from contextlib import ExitStack

import concourse.mybir as mybir
from concourse.masks import make_identity

K, T, E, C, N = 1536, 1024, 8, 128, 512
FLOPS = 2 * K * E * C * N
BYTES = 4 * K * T + E * K * N + E * (K // 32) * N + 4 * N * E + 4 * E * C + 2 * 2 * 128 * (E * C // 16) + 4 * N * T

F32 = mybir.dt.float32
BF16 = mybir.dt.bfloat16
I32 = mybir.dt.int32
U32 = mybir.dt.uint32
U16 = mybir.dt.uint16
U8 = mybir.dt.uint8
FP8X4 = mybir.dt.float8_e4m3fn_x4
RELU = mybir.ActivationFunctionType.Relu
SQUARE = mybir.ActivationFunctionType.Square
COPY = mybir.ActivationFunctionType.Copy
MULT = mybir.AluOpType.mult

P = 128
PASSES = K // 512
BLOCKS = N // P
BLOCK_BYTES = 4 * P

LOADS = ((1024,), (512, 512), (512, 512))
QUANTS = ((512, 256, 256), (512, 256, 256), (512, 256, 256))
VECTOR_COLUMNS = (((0, 512),(896,1024)), ((832, 1024),), ((832, 1024),))
EARLY_GATHERS = [range(0, 2), range(2, E)]
LATE_GATHERS = [range(0, 1), range(1, 2), range(2, 5), range(5, E)]

TOKEN_START = (8, 12, 0)
RUNS = [range(first, first + 4) for nine in range(0, E * PASSES, 9) for first in (nine, nine + 4) if first + 4 <= E * PASSES]
LEFT_OVER = [range(8, 18, 9), range(22, 24)]
PLANE_TILES = sorted(RUNS + LEFT_OVER, key=lambda planes: planes.start)

WHOLE = E // 2
STEPS = [(range(BLOCKS), range(e, e + 1)) for e in range(WHOLE)] + [
    (range(g, g + 2), range(e, e + 2)) for g in (0, 2) for e in range(WHOLE, E, 2)
]
LAST = len(STEPS) - 1
SHARED = 256
BEHIND = {
    2: (1, range(0, SHARED)),
    3: (3, range(0, 2 * C)),
    4: (3, range(2 * C, 4 * C)),
    5: (1, range(4 * C, 4 * C + 256)),
    7: (3, range(4 * C, 6 * C)),
}
SPARE = 8
POOL_SQUARES = range(2, 6)
UPPER_FIRST = (6,)
TWO_BANKS = range(len(STEPS))
WORK_BUFS = 4
PSUM_BANKS = 8


def spans(widths):
    ends = [sum(widths[: n + 1]) for n in range(len(widths))]
    return list(zip([0] + ends[:-1], ends))


def tile_moe_two_lin_relu2_kernel(tc, xT, w_words, w_scales, b, gate, offs, dst, out):
    nc = tc.nc
    with ExitStack() as ctx:
        lists = ctx.enter_context(tc.tile_pool(name="lists", bufs=1))
        keep = ctx.enter_context(tc.tile_pool(name="keep", bufs=1))
        work = ctx.enter_context(tc.tile_pool(name="work", bufs=WORK_BUFS))
        psum = ctx.enter_context(tc.psum_pool(name="psum", bufs=1))

        offs_t = lists.tile([P, T // 16], U16, name="offs_t")
        dst_t = lists.tile([P, T // 16], U16, name="dst_t")

        w_sc = []
        for n in range(len(PLANE_TILES)):
            planes_tile = keep.tile([P, N], U8, name="w_sc%d" % n, align_bytes=64)
            nc.vector.memset(planes_tile[:].bitcast(I32), 0)
            w_sc.append(planes_tile)
        x_sc = keep.tile([P, T], U8, name="x_sc", align_bytes=64)
        nc.vector.memset(x_sc[:].bitcast(I32), 0)

        identity = keep.tile([P, P], F32, name="identity")
        make_identity(nc, identity[:])
        bias_rows = keep.tile([P, 3 * E + P], F32, name="bias_rows")
        nc.gpsimd.memset(bias_rows[:, 4 * E :], 0.0)
        gate_rows = keep.tile([P, E], F32, name="gate_rows")

        x_view = xT.rearrange("(a p j) w -> a p j w", p=P, j=4)
        raws = {}
        for a in range(PASSES):
            for lo, hi in spans(LOADS[a]):
                raw = keep.tile([P, 4, hi - lo], F32, name="raw%d_%d" % (a, lo))
                nc.sync.dma_start(out=raw[:], in_=x_view[a, :, :, lo:hi])
                raws[a, lo] = raw
            if a == 0:
                nc.sync.dma_start(offs_t[:], offs)
        nc.sync.dma_start(out=bias_rows[:, 0 : 4 * E], in_=b.rearrange("(p j) e -> p (j e)", j=4))
        nc.sync.dma_start(out=gate_rows[:], in_=gate[0, :].rearrange("(k r) -> k r", r=E))

        sc_view = w_scales.rearrange("e a q n -> (e a) q n")
        homes = {plane: (n, 4 * j) for n, planes in enumerate(PLANE_TILES) for j, plane in enumerate(planes)}
        w_view = w_words.rearrange("e a p n r -> p (e a) (n r)")
        w_tiles = []
        for n, (rows, experts) in enumerate(STEPS):
            if n < len(PLANE_TILES):
                planes = PLANE_TILES[n]
                for quadrant in range(4):
                    nc.sync.dma_start(
                        out=w_sc[n][32 * quadrant : 32 * quadrant + 4 * len(planes), :].bitcast(I32),
                        in_=sc_view[planes.start : planes.stop : planes.step, 4 * quadrant : 4 * quadrant + 4, :].bitcast(I32),
                    )
            source = w_view[
                :, PASSES * experts.start : PASSES * experts.stop, BLOCK_BYTES * rows.start : BLOCK_BYTES * rows.stop
            ]
            words = keep.tile(list(source.shape), U8, name="w%d" % n, align_bytes=64)
            nc.sync.dma_start(out=words[:].bitcast(I32), in_=source.bitcast(I32))
            w_tiles.append(words)
            if n == 2:
                nc.sync.dma_start(dst_t[:], dst)

        codes = [keep.tile([P, T], U32, name="codes%d" % a, align_bytes=64) for a in range(PASSES)]
        g_words = [keep.tile([P, T], U32, name="g_words%d" % a, align_bytes=64) for a in range(PASSES)]
        g_bytes = keep.tile([P, T], U8, name="g_bytes", align_bytes=64)

        def slots(experts):
            return slice(C * experts.start, C * experts.stop)

        def entries(list_tile, experts):
            return list_tile[:, C * experts.start // 16 : C * experts.stop // 16]

        def gather(gathered, window, experts):
            nc.vector.tensor_copy(gathered[:, slots(experts)], window[:].indirect(entries(offs_t, experts)))

        for a in range(PASSES):
            grouped = {
                c0: keep.tile([P, c1 - c0, 4], BF16, name="grouped%d_%d" % (a, c0), align_bytes=64) for c0, c1 in spans(QUANTS[a])
            }
            cuts = sorted(set([lo for lo, hi in spans(LOADS[a])] + [T] + list(grouped) + [x for span in VECTOR_COLUMNS[a] for x in span]))
            for lo, hi in spans(LOADS[a]):
                for x0, x1 in zip(cuts, cuts[1:]):
                    if lo <= x0 < hi:
                        on_vector = any(first <= x0 < last for first, last in VECTOR_COLUMNS[a])
                        copy = nc.vector.tensor_copy if on_vector else nc.scalar.copy
                        c0 = max(c for c in grouped if c <= x0)
                        copy(
                            grouped[c0][:, x0 - c0 : x1 - c0, :].rearrange("p (c i) t -> p c t i", i=4),
                            raws[a, lo][:, :, x0 - lo : x1 - lo].rearrange("p t (c i) -> p c t i", i=4),
                        )
                for c0, c1 in spans(QUANTS[a]):
                    if lo < c1 <= hi:
                        nc.vector.quantize_mx(
                            out=codes[a][:, c0:c1].bitcast(FP8X4),
                            scales=x_sc[TOKEN_START[a] : P, c0:c1],
                            in_=grouped[c0][:].rearrange("p w j -> p (w j)"),
                        )
            if a < PASSES - 1:
                for experts in EARLY_GATHERS:
                    gather(g_words[a], codes[a], experts)
        for experts in LATE_GATHERS:
            gather(g_words[PASSES - 1], codes[PASSES - 1], experts)
            gather(g_bytes, x_sc, experts)

        turned = psum.tile([P, 4, P], F32, name="bank", bufs=PSUM_BANKS)
        for j in range(4):
            nc.tensor.transpose(turned[:, j, :], bias_rows[:, E * j : E * j + P], identity[:])
        by_expert = keep.tile([P, P, 4], F32, name="by_expert")
        nc.scalar.copy(by_expert[:], turned[:].rearrange("e j p -> e p j"))
        spread = []
        for h in range(2):
            four = psum.tile([P, 4, P], F32, name="bank", bufs=PSUM_BANKS)
            for r in range(4):
                nc.tensor.transpose(four[:, r, :], gate_rows[:, 4 * h + r : 4 * h + r + 1].to_broadcast([P, P]), identity[:])
            spread.append(four)
        back = psum.tile([P, BLOCKS, P], F32, name="bank", bufs=PSUM_BANKS)
        for g in range(BLOCKS):
            nc.tensor.transpose(back[:, g, :], by_expert[:].rearrange("e p j -> e (p j)")[:, P * g : P * (g + 1)], identity[:])
        gate_t = keep.tile([P, T], F32, name="gate_t")
        for h in range(2):
            nc.scalar.copy(
                gate_t[:].rearrange("p (k r) -> p k r", r=E)[:, :, 4 * h : 4 * h + 4], spread[h][:].rearrange("p r k -> p k r")
            )
        bias = keep.tile([P, BLOCKS, E], F32, name="bias")
        nc.scalar.copy(bias[:], back[:, :, 0:E])

        windows = [keep.tile([P, T + SPARE * (g % 2)], F32, name="window%d" % g) for g in range(BLOCKS)]
        gated = keep.tile([P, BLOCKS, T], F32, name="gated")

        def products(n, rows):
            experts = STEPS[n][1]
            bank = psum.tile([P, len(rows), len(experts), C], F32, name="bank", bufs=PSUM_BANKS)
            for u, g in enumerate(rows):
                first = BLOCK_BYTES * (g - STEPS[n][0].start)
                for v, e in enumerate(experts):
                    for a in range(PASSES):
                        home, start = homes[PASSES * e + a]
                        nc.tensor.matmul_mx(
                            out=bank[:, u, v, :],
                            lhsT=w_tiles[n][:, PASSES * v + a, first : first + BLOCK_BYTES].bitcast(FP8X4),
                            lhsT_scale=w_sc[home][start:P, P * g : P * (g + 1)],
                            rhs=g_words[a][:, C * e : C * (e + 1)].bitcast(FP8X4),
                            rhs_scale=g_bytes[TOKEN_START[a] : P, C * e : C * (e + 1)],
                            start=(a == 0),
                            stop=(a == PASSES - 1),
                        )
            return bank

        def halves_of(n):
            rows = STEPS[n][0]
            half = len(rows) // 2
            return [rows[half:], rows[:half]] if n in UPPER_FIRST else [rows[:half], rows[half:]]

        last_bias = {}
        for n, (g, scattered_experts) in BEHIND.items():
            place = T + len([m for m in last_bias if BEHIND[m][0] == g])
            last_bias[n] = windows[g][:, place : place + 1]
            e = STEPS[n][1][-1]
            nc.scalar.copy(last_bias[n], back[:, halves_of(n)[1][-1], e : e + 1])

        def prepare(n):
            rows, experts = STEPS[n]
            halves = halves_of(n)
            shape = [P, len(halves[0]), C * len(experts)]
            relu = [work.tile(shape, F32, name="relu%d" % h) for h in range(2)]
            in_order = list(halves[0]) + list(halves[1])
            groups = halves if n in TWO_BANKS else [in_order]
            for group in [[g] for g in in_order] if n in range(WHOLE) else groups:
                bank = products(n, group)
                for u, g in enumerate(group):
                    h, place = divmod(in_order.index(g), shape[1])
                    for v, e in enumerate(experts):
                        last = n in BEHIND and g == in_order[-1] and e == experts[-1]
                        nc.scalar.activation(
                            relu[h][:, place, C * v : C * (v + 1)],
                            bank[:, u, v, :],
                            RELU,
                            bias=last_bias[n] if last else bias[:, g, e : e + 1],
                        )
            gates = gate_t[:, slots(experts)].unsqueeze(1).to_broadcast(shape)
            values = [gated[:, h.start : h.stop, slots(experts)] for h in halves]
            factors = [work.tile(shape, F32, name="factor%d" % h) for h in range(2)]
            nc.scalar.activation(factors[0][:], relu[0][:], SQUARE)
            if n in POOL_SQUARES:
                nc.gpsimd.tensor_tensor(factors[1][:], relu[1][:], gates, MULT)
            else:
                nc.scalar.activation(factors[1][:], relu[1][:], SQUARE)
            nc.gpsimd.tensor_tensor(values[0], factors[0][:], gates, MULT)
            nc.gpsimd.tensor_tensor(values[1], factors[1][:], relu[1][:] if n in POOL_SQUARES else gates, MULT)

        scattered = {g: [] for g in range(BLOCKS)}

        def scatter(g, taken, by_scalar):
            values = gated[:, g, taken.start : taken.stop]
            places = windows[g][:].indirect(dst_t[:, taken.start // 16 : taken.stop // 16])
            if by_scalar:
                nc.scalar.activation(places, values, COPY)
            else:
                nc.vector.tensor_copy(places, values)
            scattered[g].extend(taken)
            if len(scattered[g]) == T:
                queue = nc.scalar if g == BLOCKS - 1 else nc.sync
                queue.dma_start(out=out[P * g : P * (g + 1), :], in_=windows[g][:, 0:T])

        for n, (rows, experts) in enumerate(STEPS):
            prepare(n)
            if n in BEHIND:
                scatter(BEHIND[n][0], BEHIND[n][1], True)
            if n == WHOLE - 1:
                scatter(1, range(SHARED, WHOLE * C), False)
            for g in rows if n == 5 else rows[::2]:
                scatter(g, range(C * experts.start, C * experts.stop), False)
        scatter(BLOCKS - 1, range(6 * C, T), True)
